import numpy as np
import ml_dtypes


def mxq(x, axis, fmt="e4m3"):
    dtype, down = {"e4m3": (ml_dtypes.float8_e4m3fn, 7), "e5m2": (ml_dtypes.float8_e5m2, 14)}[fmt]
    v = np.moveaxis(np.asarray(x, np.float32).astype(ml_dtypes.bfloat16).astype(np.float64), axis, -1)
    blocks = v.reshape(v.shape[:-1] + (-1, 32))
    amax = np.abs(blocks).max(-1, keepdims=True)
    byte = np.maximum(np.where(amax > 0, np.frexp(amax)[1] - 1 + 127, 0) - down, 1)
    scale = np.exp2(byte - 127.0)
    codes = (blocks / scale).astype(np.float32).astype(dtype).astype(np.float64)
    return np.moveaxis((codes * scale).reshape(v.shape), -1, axis)


WIDE = False


def mx_kscale(k):
    if not WIDE:
        return np.ones(k)
    levels = np.array([10, -10, 5, -5, 0])
    if k % 512:
        return np.exp2(np.random.permutation(np.resize(levels, k // 32))).repeat(32)
    a = np.empty((k // 512, 16))
    for p in range(k // 512):
        a[p, :8] = np.random.permutation(np.resize(levels, 8))
        for g in range(8):
            far = levels[np.abs(levels - a[p, g]) >= 10]
            a[p, g + 8] = far[np.random.randint(len(far))]
    return np.exp2(a.ravel()).repeat(32)


def f64(x):
    return np.asarray(x).astype(np.float64)


def striped(idx):
    return np.tile(idx.reshape(-1, 16).T, (8, 1)).astype(np.uint16)


def unstriped(offs):
    return offs[:16].T.reshape(-1).astype(np.int64)


E2M1 = np.array([0.0, 0.5, 1.0, 1.5, 2.0, 3.0, 4.0, 6.0, -0.0, -0.5, -1.0, -1.5, -2.0, -3.0, -4.0, -6.0])


def pack_weight(w, fmt):
    k, n = w.shape
    w = f64(np.asarray(w, np.float32).astype(ml_dtypes.bfloat16)).reshape(k // 32, 32, n)
    amax = np.abs(w).max(1)
    if fmt == "e4m3":
        byte = np.frexp(amax)[1] - 1 + 127 - 7
    else:
        mant, ex = np.frexp(amax / 6.0)
        byte = np.where(mant > 0.5, ex, ex - 1) + 127
    byte = np.clip(np.where(amax > 0, byte, 1), 1, 254)
    scaled = (w * np.exp2(127.0 - byte)[:, None, :]).reshape(k, n).astype(np.float32)
    by_word = np.ascontiguousarray(scaled.reshape(k // 512, 128, 4, n).transpose(0, 1, 3, 2))
    if fmt == "e4m3":
        words = by_word.astype(ml_dtypes.float8_e4m3fn).view(np.uint8)
    else:
        c = by_word.astype(ml_dtypes.float4_e2m1fn).view(np.uint8) & 0xF
        words = (c[..., 0::2] | (c[..., 1::2] << 4)).reshape(k // 512, 128, 2 * n)
    return np.ascontiguousarray(words), np.ascontiguousarray(byte.astype(np.uint8).reshape(k // 512, 16, n))


def unpack_weight(words, scales, fmt):
    g, _, n = scales.shape
    words = np.ascontiguousarray(words).reshape(g, 128, n, -1)
    if fmt == "e4m3":
        vals = words.view(ml_dtypes.float8_e4m3fn).astype(np.float64)
    else:
        nib = np.empty((g, 128, n, 4), np.uint8)
        nib[..., 0::2] = words & 0xF
        nib[..., 1::2] = words >> 4
        vals = E2M1[nib]
    vals = vals * np.repeat(np.exp2(scales.astype(np.float64) - 127.0), 8, axis=1)[..., None]
    return vals.transpose(0, 1, 3, 2).reshape(g * 512, n)


def gelu(v):
    return 0.5 * v * (1.0 + np.tanh(np.sqrt(2.0 / np.pi) * (v + 0.044715 * v**3)))


K, T, E, C, H, N = 1024, 512, 8, 128, 512, 128


def by_expert(wq, xq):
    return np.concatenate([wq[e].T @ xq[:, e * C:(e + 1) * C] for e in range(E)], axis=1)


def setup_inputs():
    n = np.random.standard_normal
    s = mx_kscale(K)
    u = mx_kscale(H)
    first = np.random.permutation(np.repeat(np.arange(E), T // E))
    second = (first + 1 + np.random.permutation(np.repeat(np.arange(E - 1), -(-T // (E - 1)))[:T])) % E
    while np.bincount(second, minlength=E).max() != T // E:
        load = np.bincount(second, minlength=E); hi, lo = int(load.argmax()), int(load.argmin())
        t = np.flatnonzero((second == hi) & (first != lo))[0]; second[t] = lo
    slot_token = np.empty(E * C, np.int64); pos = np.empty((2, T), np.int64); fill = np.zeros(E, np.int64)
    place = np.stack([np.random.permutation(C) for _ in range(E)])
    for r, deal in enumerate((first, second)):
        for t in np.random.permutation(T):
            e = deal[t]; j = e * C + place[e, fill[e]]; fill[e] += 1; slot_token[j] = t; pos[r, t] = j
    g = np.random.uniform(0.2, 0.8, T)
    x = pack_weight(n((K, T)) * s[:, None], "e4m3")
    wa = [pack_weight(m, "e4m3") for m in n((E, K, H)) / np.sqrt(K) / s[None, :, None] * u]
    wb = [pack_weight(m, "e4m3") for m in n((E, H, N)) / np.sqrt(H) / u[None, :, None]]
    return {
        "x_words": x[0],
        "x_scales": x[1],
        "w": (n((K, N)) / np.sqrt(K) / s[:, None]).astype(np.float32),
        "wa_words": np.stack([m[0] for m in wa]),
        "wa_scales": np.stack([m[1] for m in wa]),
        "wb_words": np.stack([m[0] for m in wb]),
        "wb_scales": np.stack([m[1] for m in wb]),
        "gate": np.stack([np.tile(g, (128, 1)), np.tile(1.0 - g, (128, 1))]).astype(np.float32),
        "offs": striped(slot_token),
        "pos1": striped(pos[0]),
        "pos2": striped(pos[1]),
    }


def reference(x_words, x_scales, w, wa_words, wa_scales, wb_words, wb_scales, gate, offs, pos1, pos2):
    wq = mxq(f64(w), 0, "e4m3")
    wa = np.stack([unpack_weight(wa_words[e], wa_scales[e], "e4m3") for e in range(E)])
    wb = np.stack([unpack_weight(wb_words[e], wb_scales[e], "e4m3") for e in range(E)])
    idx = unstriped(offs)
    x = unpack_weight(x_words, x_scales, "e4m3")
    base = wq.T @ x
    h = gelu(by_expert(wa, x[:, idx]))
    y = by_expert(wb, mxq(h, 0, "e4m3"))
    c = sum(f64(gate[r, :1]) * y[:, unstriped(p)] for r, p in enumerate((pos1, pos2)))
    return base + c

@@ -1,0 +1,225 @@
+from contextlib import ExitStack
+
+import concourse.mybir as mybir
+from concourse.masks import make_identity
+
+K, T, E, C, H, N = 1024, 512, 8, 128, 512, 128
+S = E * C
+FLOPS = 2 * K * N * T + 2 * K * H * S + 2 * H * N * S
+BYTES = K * T + K * T // 32 + 4 * K * N + E * K * H + E * K * H // 32 + E * H * N + E * H * N // 32 + 2 * 4 * T + 2 * 128 * (S + 2 * T) // 16 + 4 * N * T
+
+F32 = mybir.dt.float32
+BF16 = mybir.dt.bfloat16
+I32 = mybir.dt.int32
+U32 = mybir.dt.uint32
+U16 = mybir.dt.uint16
+U8 = mybir.dt.uint8
+FP8X4 = mybir.dt.float8_e4m3fn_x4
+GELU = mybir.ActivationFunctionType.Gelu_apprx_tanh
+MULT = mybir.AluOpType.mult
+ADD = mybir.AluOpType.add
+
+P = 128
+PASSES = K // 512
+PAIR = 2 * C
+H_GROUPS = [(0, 1), (2, 3), (4, 5), (6,), (7,)]
+Y_GROUPS = [(0, 1, 2, 3), (4, 5, 6), (7,)]
+OUT_CHUNKS = [(0, 256), (256, 512)]
+
+
+def tile_moe_adp_gelu_kernel(
+    tc, x_words, x_scales, w, wa_words, wa_scales, wb_words, wb_scales, gate, offs, pos1, pos2, out
+):
+    nc = tc.nc
+    with ExitStack() as ctx:
+        keep = ctx.enter_context(tc.tile_pool(name="keep", bufs=1))
+        psum = ctx.enter_context(tc.psum_pool(name="psum", bufs=1))
+
+        offs_t = keep.tile([P, S // 16], U16, name="offs_t")
+        pos_t = [keep.tile([P, T // 16], U16, name="pos%d_t" % r) for r in range(2)]
+        xw = [keep.tile([P, T], I32, name="xw%d" % s, align_bytes=64) for s in range(PASSES)]
+        xs = keep.tile([P, T], U8, name="xs", align_bytes=64)
+        wa_last = [keep.tile([P, H], I32, name="wa_last%d" % s, align_bytes=64) for s in range(PASSES)]
+        wa2 = [keep.tile([P, PASSES, H], I32, name="wab%d" % e, align_bytes=64) for e in range(E - 1)]
+        was = [keep.tile([P, H], U8, name="was%d" % g, align_bytes=64) for g in range(E // 2)]
+        wb = keep.tile([P, E, N], I32, name="wb", align_bytes=64)
+        wbs = keep.tile([P, E, N], U8, name="wbs", align_bytes=64)
+        w_raw = [keep.tile([P, 4, N], F32, name="w_raw%d" % s) for s in range(PASSES)]
+        gate_row = keep.tile([P, 2, 4], F32, name="gate_row")
+        gate_t = [keep.tile([P, T], F32, name="gate%d" % r) for r in range(2)]
+        ident = keep.tile([P, P], F32, name="ident")
+        warm = keep.tile([P, 8], F32, name="warm")
+
+        nc.scalar.dma_start(out=gate_row[:], in_=gate[:, 0, :].rearrange("r (p c) -> p r c", c=4))
+        make_identity(nc, ident[:])
+        nc.vector.memset(xs[:].bitcast(I32), 0)
+        for g in range(E // 2):
+            nc.vector.memset(was[g][:].bitcast(I32), 0)
+        nc.vector.memset(wbs[:].rearrange("p e n -> p (e n)").bitcast(I32), 0)
+        nc.vector.memset(warm[:], 0.0)
+        nc.scalar.activation(out=warm[:], in_=warm[:], func=GELU)
+
+        def load_x_words(s):
+            nc.sync.dma_start(out=xw[s][:], in_=x_words[s].rearrange("p t d -> p (t d)").bitcast(I32))
+
+        def load_wa(e):
+            if e < E - 1:
+                nc.sync.dma_start(out=wa2[e][:], in_=wa_words[e].rearrange("s p i d -> p s (i d)").bitcast(I32))
+            else:
+                for s in range(PASSES):
+                    nc.sync.dma_start(out=wa_last[s][:], in_=wa_words[e, s].rearrange("p i d -> p (i d)").bitcast(I32))
+
+        def wa_pass(e, s):
+            return wa2[e][:, s, :] if e < E - 1 else wa_last[s][:]
+
+        wa_planes = wa_scales.rearrange("e s b i -> (e s) b i")
+
+        def load_wa_scales(g):
+            for q in range(4):
+                nc.sync.dma_start(
+                    out=was[g][32 * q : 32 * q + 16, :].bitcast(I32),
+                    in_=wa_planes[4 * g : 4 * g + 4, 4 * q : 4 * q + 4, :].bitcast(I32),
+                )
+
+        nc.sync.dma_start(offs_t[:], offs)
+        load_x_words(0)
+        for q in range(4):
+            nc.sync.dma_start(
+                out=xs[32 * q : 32 * q + 8, :].bitcast(I32), in_=x_scales[:, 4 * q : 4 * q + 4, :].bitcast(I32)
+            )
+        load_x_words(1)
+        load_wa(0)
+        load_wa_scales(0)
+        load_wa(1)
+        for g in range(1, E // 2):
+            load_wa_scales(g)
+            load_wa(2 * g)
+            load_wa(2 * g + 1)
+        nc.sync.dma_start(out=wb[:], in_=wb_words.rearrange("e s p n d -> p (e s) (n d)").bitcast(I32))
+        nc.sync.dma_start(pos_t[0][:], pos1)
+        nc.sync.dma_start(pos_t[1][:], pos2)
+        for s in range(PASSES):
+            nc.sync.dma_start(out=w_raw[s][:], in_=w[512 * s : 512 * (s + 1), :].rearrange("(p j) n -> p j n", j=4))
+
+        for q in range(4):
+            nc.gpsimd.dma_start(
+                out=wbs[32 * q : 32 * q + 4, :, :].bitcast(I32),
+                in_=wb_scales[:, 0, 4 * q : 4 * q + 4, :].rearrange("e b n -> b e n").bitcast(I32),
+            )
+
+        for r in range(2):
+            spread = psum.tile([P, 4, P], F32, name="spread%d" % r, tag="y_acc", bufs=3)
+            for c in range(4):
+                nc.tensor.transpose(spread[:, c, :], gate_row[:, r, c : c + 1].to_broadcast([P, P]), ident[:])
+            nc.scalar.copy(out=gate_t[r][:].rearrange("q (p c) -> q p c", c=4), in_=spread[:].rearrange("q c p -> q p c"))
+
+        gw = [[keep.tile([P, PAIR], U32, name="gw%d_%d" % (g, s), align_bytes=64) for s in range(PASSES)] for g in range(E // 2)]
+        gs = [keep.tile([P, PAIR], U8, name="gs%d" % g, align_bytes=64) for g in range(E // 2)]
+        for g in range(E // 2):
+            picks = offs_t[:, g * PAIR // 16 : (g + 1) * PAIR // 16]
+            nc.vector.tensor_copy(gw[g][0][:], xw[0][:].bitcast(U32).indirect(picks))
+            nc.vector.tensor_copy(gs[g][:], xs[:].indirect(picks))
+            nc.vector.tensor_copy(gw[g][1][:], xw[1][:].bitcast(U32).indirect(picks))
+
+        h_codes, h_scales, h_slots, turned = {}, {}, {}, {}
+
+        def first_layer(e):
+            g, slots = e // 2, slice((e % 2) * C, (e % 2 + 1) * C)
+            pre = psum.tile([P, H], F32, name="pre%d" % e, tag="wide", bufs=3)
+            for s in range(PASSES):
+                plane = 4 * (2 * (e % 2) + s)
+                nc.tensor.matmul_mx(
+                    out=pre[:],
+                    lhsT=gw[g][s][:, slots].bitcast(FP8X4),
+                    lhsT_scale=gs[g][4 * s : P, slots],
+                    rhs=wa_pass(e, s).bitcast(FP8X4),
+                    rhs_scale=was[g][plane:P, :],
+                    start=(s == 0),
+                    stop=(s == PASSES - 1),
+                )
+            h_slots[e] = keep.tile([P, H], BF16, name="h_slot%d" % e, align_bytes=64)
+            nc.scalar.activation(
+                out=h_slots[e][:].rearrange("c (u m d) -> c u m d", u=2, d=2),
+                in_=pre[:].rearrange("c (m u d) -> c u m d", u=2, d=2),
+                func=GELU,
+            )
+
+        def turn(e):
+            group = [grp for grp in H_GROUPS if e in grp][0]
+            n_e = len(group)
+            if e == group[0]:
+                turned[group] = psum.tile([P, n_e, 2, C], F32, name="turned%d" % e, tag="turned", bufs=2)
+            h_words = h_slots[e][:].bitcast(F32)
+            for u in range(2):
+                nc.tensor.transpose(turned[group][:, e - group[0], u, :], h_words[:, u * P : (u + 1) * P], ident[:])
+            if e != group[-1]:
+                return
+            grouped = keep.tile([P, n_e * C * 4], BF16, name="grouped%d" % group[0], align_bytes=64)
+            copy_out = nc.scalar.copy if group[0] < 4 else nc.vector.tensor_copy
+            copy_out(
+                out=grouped[:].bitcast(F32).rearrange("p (a c u) -> p a c u", a=n_e, u=2),
+                in_=turned[group][:].rearrange("p a u c -> p a c u"),
+            )
+            codes = keep.tile([P, n_e * C], U32, name="h_codes%d" % group[0], align_bytes=64)
+            scales = keep.tile([P, n_e * C], U8, name="h_scales%d" % group[0], align_bytes=64)
+            nc.vector.quantize_mx(out=codes[:].bitcast(FP8X4), scales=scales[:], in_=grouped[:])
+            for a, member in enumerate(group):
+                h_codes[member] = codes[:, a * C : (a + 1) * C]
+                h_scales[member] = scales[:, a * C : (a + 1) * C]
+
+        first_layer(0)
+        for e in range(1, E):
+            first_layer(e)
+            turn(e - 1)
+        turn(E - 1)
+
+        y = keep.tile([P, S], F32, name="y")
+        for b, group in enumerate(Y_GROUPS):
+            acc = psum.tile([P, len(group) * C], F32, name="y_acc%d" % b, tag="y_acc", bufs=3)
+            for a, e in enumerate(group):
+                nc.tensor.matmul_mx(
+                    out=acc[:, a * C : (a + 1) * C],
+                    lhsT=wb[:, e, :].bitcast(FP8X4),
+                    lhsT_scale=wbs[:, e, :],
+                    rhs=h_codes[e].bitcast(FP8X4),
+                    rhs_scale=h_scales[e],
+                    start=True,
+                    stop=True,
+                )
+            cols = slice(group[0] * C, (group[-1] + 1) * C)
+            if b == 1:
+                nc.vector.tensor_copy(out=y[:, cols], in_=acc[:])
+            else:
+                nc.scalar.copy(out=y[:, cols], in_=acc[:])
+
+        w_grouped = keep.tile([P, PASSES, N, 4], BF16, name="w_grouped", align_bytes=64)
+        for s in range(PASSES):
+            nc.scalar.copy(out=w_grouped[:, s, :, :], in_=w_raw[s][:].rearrange("p j n -> p n j"))
+        w_codes = keep.tile([P, PASSES * N], U32, name="w_codes", align_bytes=64)
+        w_scales = keep.tile([P, PASSES * N], U8, name="w_scales", align_bytes=64)
+        nc.vector.quantize_mx(
+            out=w_codes[:].bitcast(FP8X4), scales=w_scales[:], in_=w_grouped[:].rearrange("p s n j -> p (s n j)")
+        )
+        base = psum.tile([P, T], F32, name="base", tag="wide", bufs=3)
+        for s in range(PASSES):
+            nc.tensor.matmul_mx(
+                out=base[:],
+                lhsT=w_codes[:, s * N : (s + 1) * N].bitcast(FP8X4),
+                lhsT_scale=w_scales[:, s * N : (s + 1) * N],
+                rhs=xw[s][:].bitcast(FP8X4),
+                rhs_scale=xs[4 * s : P, :],
+                start=(s == 0),
+                stop=(s == PASSES - 1),
+            )
+
+        parts = [[keep.tile([P, hi - lo], F32, name="part%d_%d" % (r, lo)) for r in range(2)] for lo, hi in OUT_CHUNKS]
+        for i, (lo, hi) in enumerate(OUT_CHUNKS):
+            for r in range(2):
+                nc.vector.tensor_tensor(
+                    parts[i][r][:], y[:].indirect(pos_t[r][:, lo // 16 : hi // 16]), gate_t[r][:, lo:hi], MULT
+                )
+            routed = keep.tile([P, hi - lo], F32, name="routed%d" % lo)
+            nc.vector.tensor_tensor(routed[:], parts[i][0][:], parts[i][1][:], ADD)
+            result = keep.tile([P, hi - lo], F32, name="result%d" % lo)
+            nc.vector.tensor_tensor(result[:], base[:, lo:hi], routed[:], ADD)
+            nc.sync.dma_start(out=out[:, lo:hi], in_=result[:])

@@ -22,9 +22,11 @@ ADD = mybir.AluOpType.add
 P = 128
 PASSES = K // 512
 PAIR = 2 * C
+WA_PLANES = (12, 4)
+WA_SCALE_SETS = [(0, 3), (3, E)]
 H_GROUPS = [(0, 1), (2, 3), (4, 5), (6,), (7,)]
 Y_GROUPS = [(0, 1, 2, 3), (4, 5, 6), (7,)]
-OUT_CHUNKS = [(0, 256), (256, 512)]
+OUT_CHUNKS = [(0, 384), (384, 512)]
 
 
 def tile_moe_adp_gelu_kernel(
@@ -37,30 +39,27 @@ def tile_moe_adp_gelu_kernel(
 
         offs_t = keep.tile([P, S // 16], U16, name="offs_t")
         pos_t = [keep.tile([P, T // 16], U16, name="pos%d_t" % r) for r in range(2)]
-        xw = [keep.tile([P, T], I32, name="xw%d" % s, align_bytes=64) for s in range(PASSES)]
+        xw = keep.tile([P, PASSES, T], I32, name="xw", align_bytes=64)
         xs = keep.tile([P, T], U8, name="xs", align_bytes=64)
         wa_last = [keep.tile([P, H], I32, name="wa_last%d" % s, align_bytes=64) for s in range(PASSES)]
         wa2 = [keep.tile([P, PASSES, H], I32, name="wab%d" % e, align_bytes=64) for e in range(E - 1)]
-        was = [keep.tile([P, H], U8, name="was%d" % g, align_bytes=64) for g in range(E // 2)]
+        was = [keep.tile([P, hi - lo, PASSES, H], U8, name="was%d" % lo, align_bytes=64) for lo, hi in WA_SCALE_SETS]
         wb = keep.tile([P, E, N], I32, name="wb", align_bytes=64)
         wbs = keep.tile([P, E, N], U8, name="wbs", align_bytes=64)
-        w_raw = [keep.tile([P, 4, N], F32, name="w_raw%d" % s) for s in range(PASSES)]
+        w_raw = keep.tile([P, PASSES, 4, N], F32, name="w_raw")
         gate_row = keep.tile([P, 2, 4], F32, name="gate_row")
         gate_t = [keep.tile([P, T], F32, name="gate%d" % r) for r in range(2)]
         ident = keep.tile([P, P], F32, name="ident")
         warm = keep.tile([P, 8], F32, name="warm")
 
-        nc.scalar.dma_start(out=gate_row[:], in_=gate[:, 0, :].rearrange("r (p c) -> p r c", c=4))
+        nc.gpsimd.memset(xs[:].bitcast(I32), 0)
+        nc.gpsimd.dma_start(out=gate_row[:], in_=gate[:, 0, :].rearrange("r (p c) -> p r c", c=4))
         make_identity(nc, ident[:])
-        nc.vector.memset(xs[:].bitcast(I32), 0)
-        for g in range(E // 2):
-            nc.vector.memset(was[g][:].bitcast(I32), 0)
+        for a in range(2):
+            nc.vector.memset(was[a][:].rearrange("p e s i -> p (e s i)").bitcast(I32), 0)
         nc.vector.memset(wbs[:].rearrange("p e n -> p (e n)").bitcast(I32), 0)
         nc.vector.memset(warm[:], 0.0)
         nc.scalar.activation(out=warm[:], in_=warm[:], func=GELU)
-
-        def load_x_words(s):
-            nc.sync.dma_start(out=xw[s][:], in_=x_words[s].rearrange("p t d -> p (t d)").bitcast(I32))
 
         def load_wa(e):
             if e < E - 1:
@@ -72,91 +71,92 @@ def tile_moe_adp_gelu_kernel(
         def wa_pass(e, s):
             return wa2[e][:, s, :] if e < E - 1 else wa_last[s][:]
 
-        wa_planes = wa_scales.rearrange("e s b i -> (e s) b i")
-
-        def load_wa_scales(g):
+        def load_wa_scales(a, queue):
+            lo, hi = WA_SCALE_SETS[a]
             for q in range(4):
-                nc.sync.dma_start(
-                    out=was[g][32 * q : 32 * q + 16, :].bitcast(I32),
-                    in_=wa_planes[4 * g : 4 * g + 4, 4 * q : 4 * q + 4, :].bitcast(I32),
+                row = 32 * q + WA_PLANES[a]
+                queue.dma_start(
+                    out=was[a][row : row + 4, :, :, :].rearrange("b e s i -> b (e s) i").bitcast(I32),
+                    in_=wa_scales[lo:hi, :, 4 * q : 4 * q + 4, :].rearrange("e s b i -> b (e s) i").bitcast(I32),
                 )
 
-        nc.sync.dma_start(offs_t[:], offs)
-        load_x_words(0)
+        nc.sync.dma_start(out=xw[:], in_=x_words.rearrange("s p t d -> p s (t d)").bitcast(I32))
         for q in range(4):
             nc.sync.dma_start(
                 out=xs[32 * q : 32 * q + 8, :].bitcast(I32), in_=x_scales[:, 4 * q : 4 * q + 4, :].bitcast(I32)
             )
-        load_x_words(1)
+        nc.sync.dma_start(offs_t[:], offs)
         load_wa(0)
-        load_wa_scales(0)
-        load_wa(1)
-        for g in range(1, E // 2):
-            load_wa_scales(g)
-            load_wa(2 * g)
-            load_wa(2 * g + 1)
-        nc.sync.dma_start(out=wb[:], in_=wb_words.rearrange("e s p n d -> p (e s) (n d)").bitcast(I32))
-        nc.sync.dma_start(pos_t[0][:], pos1)
-        nc.sync.dma_start(pos_t[1][:], pos2)
-        for s in range(PASSES):
-            nc.sync.dma_start(out=w_raw[s][:], in_=w[512 * s : 512 * (s + 1), :].rearrange("(p j) n -> p j n", j=4))
-
+        load_wa_scales(0, nc.sync)
+        load_wa_scales(1, nc.gpsimd)
         for q in range(4):
             nc.gpsimd.dma_start(
                 out=wbs[32 * q : 32 * q + 4, :, :].bitcast(I32),
                 in_=wb_scales[:, 0, 4 * q : 4 * q + 4, :].rearrange("e b n -> b e n").bitcast(I32),
             )
+        for e in range(1, E):
+            load_wa(e)
+        nc.sync.dma_start(
+            out=w_raw[:].rearrange("p s j n -> p s (j n)"), in_=w.rearrange("(s p j) n -> p s (j n)", s=PASSES, j=4)
+        )
+        nc.sync.dma_start(out=wb[:], in_=wb_words.rearrange("e s p n d -> p (e s) (n d)").bitcast(I32))
+        nc.sync.dma_start(pos_t[0][:], pos1)
+        nc.sync.dma_start(pos_t[1][:], pos2)
 
         for r in range(2):
-            spread = psum.tile([P, 4, P], F32, name="spread%d" % r, tag="y_acc", bufs=3)
+            spread = psum.tile([P, 4, P], F32, name="spread%d" % r, tag="turned", bufs=3)
             for c in range(4):
                 nc.tensor.transpose(spread[:, c, :], gate_row[:, r, c : c + 1].to_broadcast([P, P]), ident[:])
             nc.scalar.copy(out=gate_t[r][:].rearrange("q (p c) -> q p c", c=4), in_=spread[:].rearrange("q c p -> q p c"))
 
         gw = [[keep.tile([P, PAIR], U32, name="gw%d_%d" % (g, s), align_bytes=64) for s in range(PASSES)] for g in range(E // 2)]
         gs = [keep.tile([P, PAIR], U8, name="gs%d" % g, align_bytes=64) for g in range(E // 2)]
-        for g in range(E // 2):
-            picks = offs_t[:, g * PAIR // 16 : (g + 1) * PAIR // 16]
-            nc.vector.tensor_copy(gw[g][0][:], xw[0][:].bitcast(U32).indirect(picks))
-            nc.vector.tensor_copy(gs[g][:], xs[:].indirect(picks))
-            nc.vector.tensor_copy(gw[g][1][:], xw[1][:].bitcast(U32).indirect(picks))
+        for e in range(E):
+            g, slots = e // 2, slice((e % 2) * C, (e % 2 + 1) * C)
+            picks = offs_t[:, e * C // 16 : (e + 1) * C // 16]
+            nc.vector.tensor_copy(gw[g][0][:, slots], xw[:, 0, :].bitcast(U32).indirect(picks))
+            if e % 2 == 0:
+                nc.vector.tensor_copy(gs[g][:], xs[:].indirect(offs_t[:, g * PAIR // 16 : (g + 1) * PAIR // 16]))
+            nc.vector.tensor_copy(gw[g][1][:, slots], xw[:, 1, :].bitcast(U32).indirect(picks))
 
         h_codes, h_scales, h_slots, turned = {}, {}, {}, {}
 
         def first_layer(e):
             g, slots = e // 2, slice((e % 2) * C, (e % 2 + 1) * C)
-            pre = psum.tile([P, H], F32, name="pre%d" % e, tag="wide", bufs=3)
+            pre = psum.tile([P, H], F32, name="pre%d" % e, tag="wide", bufs=4)
             for s in range(PASSES):
-                plane = 4 * (2 * (e % 2) + s)
+                a = 0 if e < WA_SCALE_SETS[0][1] else 1
+                plane = WA_PLANES[a]
                 nc.tensor.matmul_mx(
                     out=pre[:],
                     lhsT=gw[g][s][:, slots].bitcast(FP8X4),
                     lhsT_scale=gs[g][4 * s : P, slots],
                     rhs=wa_pass(e, s).bitcast(FP8X4),
-                    rhs_scale=was[g][plane:P, :],
+                    rhs_scale=was[a][plane:P, e - WA_SCALE_SETS[a][0], s, :],
                     start=(s == 0),
                     stop=(s == PASSES - 1),
                 )
             h_slots[e] = keep.tile([P, H], BF16, name="h_slot%d" % e, align_bytes=64)
-            nc.scalar.activation(
-                out=h_slots[e][:].rearrange("c (u m d) -> c u m d", u=2, d=2),
-                in_=pre[:].rearrange("c (m u d) -> c u m d", u=2, d=2),
-                func=GELU,
-            )
+            h_view = h_slots[e][:].rearrange("c (u m d) -> c u m d", u=2, d=2)
+            pre_view = pre[:].rearrange("c (m u d) -> c u m d", u=2, d=2)
+            if e < E - 1:
+                nc.scalar.activation(out=h_view, in_=pre_view, func=GELU)
+            else:
+                for u in range(2):
+                    nc.scalar.activation(out=h_view[:, u, :, :], in_=pre_view[:, u, :, :], func=GELU)
 
         def turn(e):
             group = [grp for grp in H_GROUPS if e in grp][0]
             n_e = len(group)
             if e == group[0]:
-                turned[group] = psum.tile([P, n_e, 2, C], F32, name="turned%d" % e, tag="turned", bufs=2)
+                turned[group] = psum.tile([P, n_e, 2, C], F32, name="turned%d" % e, tag="turned", bufs=3)
             h_words = h_slots[e][:].bitcast(F32)
             for u in range(2):
                 nc.tensor.transpose(turned[group][:, e - group[0], u, :], h_words[:, u * P : (u + 1) * P], ident[:])
             if e != group[-1]:
                 return
             grouped = keep.tile([P, n_e * C * 4], BF16, name="grouped%d" % group[0], align_bytes=64)
-            copy_out = nc.scalar.copy if group[0] < 4 else nc.vector.tensor_copy
-            copy_out(
+            nc.vector.tensor_copy(
                 out=grouped[:].bitcast(F32).rearrange("p (a c u) -> p a c u", a=n_e, u=2),
                 in_=turned[group][:].rearrange("p a u c -> p a c u"),
             )
@@ -175,7 +175,7 @@ def tile_moe_adp_gelu_kernel(
 
         y = keep.tile([P, S], F32, name="y")
         for b, group in enumerate(Y_GROUPS):
-            acc = psum.tile([P, len(group) * C], F32, name="y_acc%d" % b, tag="y_acc", bufs=3)
+            acc = psum.tile([P, len(group) * C], F32, name="y_acc%d" % b, tag="wide", bufs=4)
             for a, e in enumerate(group):
                 nc.tensor.matmul_mx(
                     out=acc[:, a * C : (a + 1) * C],
@@ -194,19 +194,19 @@ def tile_moe_adp_gelu_kernel(
 
         w_grouped = keep.tile([P, PASSES, N, 4], BF16, name="w_grouped", align_bytes=64)
         for s in range(PASSES):
-            nc.scalar.copy(out=w_grouped[:, s, :, :], in_=w_raw[s][:].rearrange("p j n -> p n j"))
+            nc.scalar.copy(out=w_grouped[:, s, :, :], in_=w_raw[:, s, :, :].rearrange("p j n -> p n j"))
         w_codes = keep.tile([P, PASSES * N], U32, name="w_codes", align_bytes=64)
         w_scales = keep.tile([P, PASSES * N], U8, name="w_scales", align_bytes=64)
         nc.vector.quantize_mx(
             out=w_codes[:].bitcast(FP8X4), scales=w_scales[:], in_=w_grouped[:].rearrange("p s n j -> p (s n j)")
         )
-        base = psum.tile([P, T], F32, name="base", tag="wide", bufs=3)
+        base = psum.tile([P, T], F32, name="base", tag="base", bufs=1)
         for s in range(PASSES):
             nc.tensor.matmul_mx(
                 out=base[:],
                 lhsT=w_codes[:, s * N : (s + 1) * N].bitcast(FP8X4),
                 lhsT_scale=w_scales[:, s * N : (s + 1) * N],
-                rhs=xw[s][:].bitcast(FP8X4),
+                rhs=xw[:, s, :].bitcast(FP8X4),
                 rhs_scale=xs[4 * s : P, :],
                 start=(s == 0),
                 stop=(s == PASSES - 1),

@@ -53,8 +53,8 @@ def tile_moe_adp_gelu_kernel(
         warm = keep.tile([P, 8], F32, name="warm")
 
         nc.gpsimd.memset(xs[:].bitcast(I32), 0)
-        nc.gpsimd.dma_start(out=gate_row[:], in_=gate[:, 0, :].rearrange("r (p c) -> p r c", c=4))
         make_identity(nc, ident[:])
+        nc.gpsimd.dma_start(out=gate_row[:], in_=gate[:, 0, :].rearrange("r (p c) -> p r c", c=4))
         for a in range(2):
             nc.vector.memset(was[a][:].rearrange("p e s i -> p (e s i)").bitcast(I32), 0)
         nc.vector.memset(wbs[:].rearrange("p e n -> p (e n)").bitcast(I32), 0)
@@ -71,11 +71,11 @@ def tile_moe_adp_gelu_kernel(
         def wa_pass(e, s):
             return wa2[e][:, s, :] if e < E - 1 else wa_last[s][:]
 
-        def load_wa_scales(a, queue):
+        def load_wa_scales(a):
             lo, hi = WA_SCALE_SETS[a]
             for q in range(4):
                 row = 32 * q + WA_PLANES[a]
-                queue.dma_start(
+                nc.sync.dma_start(
                     out=was[a][row : row + 4, :, :, :].rearrange("b e s i -> b (e s) i").bitcast(I32),
                     in_=wa_scales[lo:hi, :, 4 * q : 4 * q + 4, :].rearrange("e s b i -> b (e s) i").bitcast(I32),
                 )
@@ -87,19 +87,20 @@ def tile_moe_adp_gelu_kernel(
             )
         nc.sync.dma_start(offs_t[:], offs)
         load_wa(0)
-        load_wa_scales(0, nc.sync)
-        load_wa_scales(1, nc.gpsimd)
+        load_wa_scales(0)
+        load_wa(1)
+        load_wa_scales(1)
+        for e in range(2, E):
+            load_wa(e)
+        nc.sync.dma_start(out=wb[:], in_=wb_words.rearrange("e s p n d -> p (e s) (n d)").bitcast(I32))
         for q in range(4):
-            nc.gpsimd.dma_start(
+            nc.sync.dma_start(
                 out=wbs[32 * q : 32 * q + 4, :, :].bitcast(I32),
                 in_=wb_scales[:, 0, 4 * q : 4 * q + 4, :].rearrange("e b n -> b e n").bitcast(I32),
             )
-        for e in range(1, E):
-            load_wa(e)
         nc.sync.dma_start(
             out=w_raw[:].rearrange("p s j n -> p s (j n)"), in_=w.rearrange("(s p j) n -> p s (j n)", s=PASSES, j=4)
         )
-        nc.sync.dma_start(out=wb[:], in_=wb_words.rearrange("e s p n d -> p (e s) (n d)").bitcast(I32))
         nc.sync.dma_start(pos_t[0][:], pos1)
         nc.sync.dma_start(pos_t[1][:], pos2)
 
@@ -156,7 +157,8 @@ def tile_moe_adp_gelu_kernel(
             if e != group[-1]:
                 return
             grouped = keep.tile([P, n_e * C * 4], BF16, name="grouped%d" % group[0], align_bytes=64)
-            nc.vector.tensor_copy(
+            copy_out = nc.scalar.copy if group[0] in (0, E - 1) else nc.vector.tensor_copy
+            copy_out(
                 out=grouped[:].bitcast(F32).rearrange("p (a c u) -> p a c u", a=n_e, u=2),
                 in_=turned[group][:].rearrange("p a u c -> p a c u"),
             )
@@ -187,14 +189,10 @@ def tile_moe_adp_gelu_kernel(
                     stop=True,
                 )
             cols = slice(group[0] * C, (group[-1] + 1) * C)
-            if b == 1:
-                nc.vector.tensor_copy(out=y[:, cols], in_=acc[:])
-            else:
-                nc.scalar.copy(out=y[:, cols], in_=acc[:])
+            nc.scalar.copy(out=y[:, cols], in_=acc[:])
 
         w_grouped = keep.tile([P, PASSES, N, 4], BF16, name="w_grouped", align_bytes=64)
-        for s in range(PASSES):
-            nc.scalar.copy(out=w_grouped[:, s, :, :], in_=w_raw[:, s, :, :].rearrange("p j n -> p n j"))
+        nc.vector.tensor_copy(out=w_grouped[:], in_=w_raw[:].rearrange("p s j n -> p s n j"))
         w_codes = keep.tile([P, PASSES * N], U32, name="w_codes", align_bytes=64)
         w_scales = keep.tile([P, PASSES * N], U8, name="w_scales", align_bytes=64)
         nc.vector.quantize_mx(

@@ -6,7 +6,7 @@ from concourse.masks import make_identity
 K, T, E, C, H, N = 1024, 512, 8, 128, 512, 128
 S = E * C
 FLOPS = 2 * K * N * T + 2 * K * H * S + 2 * H * N * S
-BYTES = K * T + K * T // 32 + 4 * K * N + E * K * H + E * K * H // 32 + E * H * N + E * H * N // 32 + 2 * 4 * T + 2 * 128 * (S + 2 * T) // 16 + 4 * N * T
+BYTES = (K * T + E * K * H + E * H * N) * 33 // 32 + 4 * K * N + 2 * 4 * T + 2 * 128 * (S + 2 * T) // 16 + 4 * N * T
 
 F32 = mybir.dt.float32
 BF16 = mybir.dt.bfloat16
@@ -20,13 +20,22 @@ MULT = mybir.AluOpType.mult
 ADD = mybir.AluOpType.add
 
 P = 128
-PASSES = K // 512
+PACK = 4
+K_PASS = P * PACK
+PASSES = K // K_PASS
+BLOCKS = K_PASS // 32
+QUADRANT = 32
+ROWS = 4
+PER_COLUMN = 16
+LAST = E - 1
 PAIR = 2 * C
-WA_PLANES = (12, 4)
-WA_SCALE_SETS = [(0, 3), (3, E)]
+HALF = E // 2
+WA_FIRST = (12, 4)
 H_GROUPS = [(0, 1), (2, 3), (4, 5), (6,), (7,)]
+SCALAR_COPIES = (H_GROUPS[0], H_GROUPS[-1])
 Y_GROUPS = [(0, 1, 2, 3), (4, 5, 6), (7,)]
-OUT_CHUNKS = [(0, 384), (384, 512)]
+OUT_CHUNKS = [(0, 384), (384, T)]
+SUM_BANKS, TURN_BANKS, BASE_BANKS = 4, 3, 1
 
 
 def tile_moe_adp_gelu_kernel(
@@ -37,187 +46,188 @@ def tile_moe_adp_gelu_kernel(
         keep = ctx.enter_context(tc.tile_pool(name="keep", bufs=1))
         psum = ctx.enter_context(tc.psum_pool(name="psum", bufs=1))
 
-        offs_t = keep.tile([P, S // 16], U16, name="offs_t")
-        pos_t = [keep.tile([P, T // 16], U16, name="pos%d_t" % r) for r in range(2)]
+        offs_t = keep.tile([P, S // PER_COLUMN], U16, name="offs_t")
+        pos_t = [keep.tile([P, T // PER_COLUMN], U16, name="pos%d_t" % r) for r in range(2)]
         xw = keep.tile([P, PASSES, T], I32, name="xw", align_bytes=64)
         xs = keep.tile([P, T], U8, name="xs", align_bytes=64)
         wa_last = [keep.tile([P, H], I32, name="wa_last%d" % s, align_bytes=64) for s in range(PASSES)]
-        wa2 = [keep.tile([P, PASSES, H], I32, name="wab%d" % e, align_bytes=64) for e in range(E - 1)]
-        was = [keep.tile([P, hi - lo, PASSES, H], U8, name="was%d" % lo, align_bytes=64) for lo, hi in WA_SCALE_SETS]
-        wb = keep.tile([P, E, N], I32, name="wb", align_bytes=64)
+        wa = [keep.tile([P, PASSES, H], I32, name="wa%d" % e, align_bytes=64) for e in range(LAST)]
+        was = [keep.tile([P, HALF, PASSES, H], U8, name="was%d" % a, align_bytes=64) for a in range(2)]
+        wb = [keep.tile([P, HALF, N], I32, name="wb%d" % a, align_bytes=64) for a in range(2)]
         wbs = keep.tile([P, E, N], U8, name="wbs", align_bytes=64)
-        w_raw = keep.tile([P, PASSES, 4, N], F32, name="w_raw")
-        gate_row = keep.tile([P, 2, 4], F32, name="gate_row")
+        w_raw = keep.tile([P, PASSES, PACK, N], F32, name="w_raw")
+        gate_row = keep.tile([P, 2, T // P], F32, name="gate_row")
         gate_t = [keep.tile([P, T], F32, name="gate%d" % r) for r in range(2)]
         ident = keep.tile([P, P], F32, name="ident")
-        warm = keep.tile([P, 8], F32, name="warm")
 
         nc.gpsimd.memset(xs[:].bitcast(I32), 0)
+        nc.gpsimd.dma_start(out=gate_row[:], in_=gate[:, 0, :].rearrange("r (p c) -> p r c", p=P))
         make_identity(nc, ident[:])
-        nc.gpsimd.dma_start(out=gate_row[:], in_=gate[:, 0, :].rearrange("r (p c) -> p r c", c=4))
         for a in range(2):
             nc.vector.memset(was[a][:].rearrange("p e s i -> p (e s i)").bitcast(I32), 0)
         nc.vector.memset(wbs[:].rearrange("p e n -> p (e n)").bitcast(I32), 0)
-        nc.vector.memset(warm[:], 0.0)
-        nc.scalar.activation(out=warm[:], in_=warm[:], func=GELU)
 
         def load_wa(e):
-            if e < E - 1:
-                nc.sync.dma_start(out=wa2[e][:], in_=wa_words[e].rearrange("s p i d -> p s (i d)").bitcast(I32))
+            if e < LAST:
+                nc.sync.dma_start(out=wa[e][:], in_=wa_words[e].rearrange("s p i d -> p s (i d)").bitcast(I32))
             else:
                 for s in range(PASSES):
                     nc.sync.dma_start(out=wa_last[s][:], in_=wa_words[e, s].rearrange("p i d -> p (i d)").bitcast(I32))
 
-        def wa_pass(e, s):
-            return wa2[e][:, s, :] if e < E - 1 else wa_last[s][:]
-
         def load_wa_scales(a):
-            lo, hi = WA_SCALE_SETS[a]
-            for q in range(4):
-                row = 32 * q + WA_PLANES[a]
+            for r in range(ROWS):
                 nc.sync.dma_start(
-                    out=was[a][row : row + 4, :, :, :].rearrange("b e s i -> b (e s) i").bitcast(I32),
-                    in_=wa_scales[lo:hi, :, 4 * q : 4 * q + 4, :].rearrange("e s b i -> b (e s) i").bitcast(I32),
+                    out=was[a][WA_FIRST[a] + r : P : QUADRANT, :, :, :].rearrange("q e s i -> q (e s) i").bitcast(I32),
+                    in_=wa_scales[HALF * a : HALF * (a + 1), :, r:BLOCKS:ROWS, :]
+                    .rearrange("e s q i -> q (e s) i")
+                    .bitcast(I32),
                 )
 
         nc.sync.dma_start(out=xw[:], in_=x_words.rearrange("s p t d -> p s (t d)").bitcast(I32))
-        for q in range(4):
+        for q in range(P // QUADRANT):
             nc.sync.dma_start(
-                out=xs[32 * q : 32 * q + 8, :].bitcast(I32), in_=x_scales[:, 4 * q : 4 * q + 4, :].bitcast(I32)
+                out=xs[QUADRANT * q : QUADRANT * q + PASSES * ROWS, :].bitcast(I32),
+                in_=x_scales[:, ROWS * q : ROWS * (q + 1), :].bitcast(I32),
             )
         nc.sync.dma_start(offs_t[:], offs)
-        load_wa(0)
-        load_wa_scales(0)
-        load_wa(1)
-        load_wa_scales(1)
+        for a in range(2):
+            load_wa(a)
+            load_wa_scales(a)
         for e in range(2, E):
             load_wa(e)
-        nc.sync.dma_start(out=wb[:], in_=wb_words.rearrange("e s p n d -> p (e s) (n d)").bitcast(I32))
-        for q in range(4):
+        for r in range(ROWS):
             nc.sync.dma_start(
-                out=wbs[32 * q : 32 * q + 4, :, :].bitcast(I32),
-                in_=wb_scales[:, 0, 4 * q : 4 * q + 4, :].rearrange("e b n -> b e n").bitcast(I32),
+                out=wbs[r:P:QUADRANT, :, :].bitcast(I32),
+                in_=wb_scales[:, 0, r:BLOCKS:ROWS, :].rearrange("e q n -> q e n").bitcast(I32),
+            )
+        for a in range(2):
+            nc.sync.dma_start(
+                out=wb[a][:],
+                in_=wb_words[HALF * a : HALF * (a + 1)].rearrange("e s p n d -> p (e s) (n d)").bitcast(I32),
             )
         nc.sync.dma_start(
-            out=w_raw[:].rearrange("p s j n -> p s (j n)"), in_=w.rearrange("(s p j) n -> p s (j n)", s=PASSES, j=4)
+            out=w_raw[:].rearrange("p s j n -> p s (j n)"), in_=w.rearrange("(s p j) n -> p s (j n)", s=PASSES, j=PACK)
         )
         nc.sync.dma_start(pos_t[0][:], pos1)
         nc.sync.dma_start(pos_t[1][:], pos2)
 
         for r in range(2):
-            spread = psum.tile([P, 4, P], F32, name="spread%d" % r, tag="turned", bufs=3)
-            for c in range(4):
+            spread = psum.tile([P, T // P, P], F32, name="spread%d" % r, tag="turn", bufs=TURN_BANKS)
+            for c in range(T // P):
                 nc.tensor.transpose(spread[:, c, :], gate_row[:, r, c : c + 1].to_broadcast([P, P]), ident[:])
-            nc.scalar.copy(out=gate_t[r][:].rearrange("q (p c) -> q p c", c=4), in_=spread[:].rearrange("q c p -> q p c"))
+            nc.vector.tensor_copy(
+                out=gate_t[r][:].rearrange("q (p c) -> q p c", p=P), in_=spread[:].rearrange("q c p -> q p c")
+            )
 
-        gw = [[keep.tile([P, PAIR], U32, name="gw%d_%d" % (g, s), align_bytes=64) for s in range(PASSES)] for g in range(E // 2)]
+        gw = [
+            [keep.tile([P, PAIR], U32, name="gw%d_%d" % (g, s), align_bytes=64) for s in range(PASSES)]
+            for g in range(E // 2)
+        ]
         gs = [keep.tile([P, PAIR], U8, name="gs%d" % g, align_bytes=64) for g in range(E // 2)]
         for e in range(E):
             g, slots = e // 2, slice((e % 2) * C, (e % 2 + 1) * C)
-            picks = offs_t[:, e * C // 16 : (e + 1) * C // 16]
+            picks = offs_t[:, e * C // PER_COLUMN : (e + 1) * C // PER_COLUMN]
             nc.vector.tensor_copy(gw[g][0][:, slots], xw[:, 0, :].bitcast(U32).indirect(picks))
             if e % 2 == 0:
-                nc.vector.tensor_copy(gs[g][:], xs[:].indirect(offs_t[:, g * PAIR // 16 : (g + 1) * PAIR // 16]))
+                pair_picks = offs_t[:, g * PAIR // PER_COLUMN : (g + 1) * PAIR // PER_COLUMN]
+                nc.vector.tensor_copy(gs[g][:], xs[:].indirect(pair_picks))
             nc.vector.tensor_copy(gw[g][1][:, slots], xw[:, 1, :].bitcast(U32).indirect(picks))
 
-        h_codes, h_scales, h_slots, turned = {}, {}, {}, {}
+        h_rows, turned, h_codes, h_scales = {}, {}, {}, {}
 
         def first_layer(e):
             g, slots = e // 2, slice((e % 2) * C, (e % 2 + 1) * C)
-            pre = psum.tile([P, H], F32, name="pre%d" % e, tag="wide", bufs=4)
+            pre = psum.tile([P, H], F32, name="pre%d" % e, tag="sum", bufs=SUM_BANKS)
             for s in range(PASSES):
-                a = 0 if e < WA_SCALE_SETS[0][1] else 1
-                plane = WA_PLANES[a]
+                words = wa[e][:, s, :] if e < LAST else wa_last[s][:]
                 nc.tensor.matmul_mx(
                     out=pre[:],
                     lhsT=gw[g][s][:, slots].bitcast(FP8X4),
-                    lhsT_scale=gs[g][4 * s : P, slots],
-                    rhs=wa_pass(e, s).bitcast(FP8X4),
-                    rhs_scale=was[a][plane:P, e - WA_SCALE_SETS[a][0], s, :],
+                    lhsT_scale=gs[g][ROWS * s : P, slots],
+                    rhs=words.bitcast(FP8X4),
+                    rhs_scale=was[e // HALF][WA_FIRST[e // HALF] : P, e % HALF, s, :],
                     start=(s == 0),
                     stop=(s == PASSES - 1),
                 )
-            h_slots[e] = keep.tile([P, H], BF16, name="h_slot%d" % e, align_bytes=64)
-            h_view = h_slots[e][:].rearrange("c (u m d) -> c u m d", u=2, d=2)
+            h_rows[e] = keep.tile([P, H], BF16, name="h_rows%d" % e, align_bytes=64)
+            h_view = h_rows[e][:].rearrange("c (u m d) -> c u m d", u=2, d=2)
             pre_view = pre[:].rearrange("c (m u d) -> c u m d", u=2, d=2)
-            if e < E - 1:
+            if e < LAST:
                 nc.scalar.activation(out=h_view, in_=pre_view, func=GELU)
             else:
                 for u in range(2):
                     nc.scalar.activation(out=h_view[:, u, :, :], in_=pre_view[:, u, :, :], func=GELU)
 
         def turn(e):
-            group = [grp for grp in H_GROUPS if e in grp][0]
-            n_e = len(group)
+            group = [members for members in H_GROUPS if e in members][0]
+            size = len(group)
             if e == group[0]:
-                turned[group] = psum.tile([P, n_e, 2, C], F32, name="turned%d" % e, tag="turned", bufs=3)
-            h_words = h_slots[e][:].bitcast(F32)
+                turned[group] = psum.tile([P, size, 2, C], F32, name="turned%d" % e, tag="turn", bufs=TURN_BANKS)
+            h_pairs = h_rows[e][:].bitcast(F32)
             for u in range(2):
-                nc.tensor.transpose(turned[group][:, e - group[0], u, :], h_words[:, u * P : (u + 1) * P], ident[:])
+                nc.tensor.transpose(turned[group][:, e - group[0], u, :], h_pairs[:, u * P : (u + 1) * P], ident[:])
             if e != group[-1]:
                 return
-            grouped = keep.tile([P, n_e * C * 4], BF16, name="grouped%d" % group[0], align_bytes=64)
-            copy_out = nc.scalar.copy if group[0] in (0, E - 1) else nc.vector.tensor_copy
+            grouped = keep.tile([P, size * C * PACK], BF16, name="grouped%d" % group[0], align_bytes=64)
+            copy_out = nc.scalar.copy if group in SCALAR_COPIES else nc.vector.tensor_copy
             copy_out(
-                out=grouped[:].bitcast(F32).rearrange("p (a c u) -> p a c u", a=n_e, u=2),
+                out=grouped[:].bitcast(F32).rearrange("p (a c u) -> p a c u", a=size, u=2),
                 in_=turned[group][:].rearrange("p a u c -> p a c u"),
             )
-            codes = keep.tile([P, n_e * C], U32, name="h_codes%d" % group[0], align_bytes=64)
-            scales = keep.tile([P, n_e * C], U8, name="h_scales%d" % group[0], align_bytes=64)
+            codes = keep.tile([P, size * C], U32, name="h_codes%d" % group[0], align_bytes=64)
+            scales = keep.tile([P, size * C], U8, name="h_scales%d" % group[0], align_bytes=64)
             nc.vector.quantize_mx(out=codes[:].bitcast(FP8X4), scales=scales[:], in_=grouped[:])
-            for a, member in enumerate(group):
-                h_codes[member] = codes[:, a * C : (a + 1) * C]
-                h_scales[member] = scales[:, a * C : (a + 1) * C]
+            for place, member in enumerate(group):
+                h_codes[member] = codes[:, place * C : (place + 1) * C]
+                h_scales[member] = scales[:, place * C : (place + 1) * C]
 
         first_layer(0)
         for e in range(1, E):
             first_layer(e)
             turn(e - 1)
-        turn(E - 1)
+        turn(LAST)
 
         y = keep.tile([P, S], F32, name="y")
-        for b, group in enumerate(Y_GROUPS):
-            acc = psum.tile([P, len(group) * C], F32, name="y_acc%d" % b, tag="wide", bufs=4)
-            for a, e in enumerate(group):
+        for group in Y_GROUPS:
+            acc = psum.tile([P, len(group) * C], F32, name="y_acc%d" % group[0], tag="sum", bufs=SUM_BANKS)
+            for place, e in enumerate(group):
                 nc.tensor.matmul_mx(
-                    out=acc[:, a * C : (a + 1) * C],
-                    lhsT=wb[:, e, :].bitcast(FP8X4),
+                    out=acc[:, place * C : (place + 1) * C],
+                    lhsT=wb[e // HALF][:, e % HALF, :].bitcast(FP8X4),
                     lhsT_scale=wbs[:, e, :],
                     rhs=h_codes[e].bitcast(FP8X4),
                     rhs_scale=h_scales[e],
                     start=True,
                     stop=True,
                 )
-            cols = slice(group[0] * C, (group[-1] + 1) * C)
-            nc.scalar.copy(out=y[:, cols], in_=acc[:])
+            nc.scalar.copy(out=y[:, group[0] * C : (group[-1] + 1) * C], in_=acc[:])
 
-        w_grouped = keep.tile([P, PASSES, N, 4], BF16, name="w_grouped", align_bytes=64)
+        w_grouped = keep.tile([P, PASSES, N, PACK], BF16, name="w_grouped", align_bytes=64)
         nc.vector.tensor_copy(out=w_grouped[:], in_=w_raw[:].rearrange("p s j n -> p s n j"))
         w_codes = keep.tile([P, PASSES * N], U32, name="w_codes", align_bytes=64)
         w_scales = keep.tile([P, PASSES * N], U8, name="w_scales", align_bytes=64)
         nc.vector.quantize_mx(
             out=w_codes[:].bitcast(FP8X4), scales=w_scales[:], in_=w_grouped[:].rearrange("p s n j -> p (s n j)")
         )
-        base = psum.tile([P, T], F32, name="base", tag="base", bufs=1)
+        base = psum.tile([P, T], F32, name="base", tag="base", bufs=BASE_BANKS)
         for s in range(PASSES):
             nc.tensor.matmul_mx(
                 out=base[:],
                 lhsT=w_codes[:, s * N : (s + 1) * N].bitcast(FP8X4),
                 lhsT_scale=w_scales[:, s * N : (s + 1) * N],
                 rhs=xw[:, s, :].bitcast(FP8X4),
-                rhs_scale=xs[4 * s : P, :],
+                rhs_scale=xs[ROWS * s : P, :],
                 start=(s == 0),
                 stop=(s == PASSES - 1),
             )
 
         parts = [[keep.tile([P, hi - lo], F32, name="part%d_%d" % (r, lo)) for r in range(2)] for lo, hi in OUT_CHUNKS]
-        for i, (lo, hi) in enumerate(OUT_CHUNKS):
+        for part, (lo, hi) in zip(parts, OUT_CHUNKS):
             for r in range(2):
-                nc.vector.tensor_tensor(
-                    parts[i][r][:], y[:].indirect(pos_t[r][:, lo // 16 : hi // 16]), gate_t[r][:, lo:hi], MULT
-                )
+                places = pos_t[r][:, lo // PER_COLUMN : hi // PER_COLUMN]
+                nc.vector.tensor_tensor(part[r][:], y[:].indirect(places), gate_t[r][:, lo:hi], MULT)
             routed = keep.tile([P, hi - lo], F32, name="routed%d" % lo)
-            nc.vector.tensor_tensor(routed[:], parts[i][0][:], parts[i][1][:], ADD)
+            nc.vector.tensor_tensor(routed[:], part[0][:], part[1][:], ADD)
             result = keep.tile([P, hi - lo], F32, name="result%d" % lo)
             nc.vector.tensor_tensor(result[:], base[:, lo:hi], routed[:], ADD)
             nc.sync.dma_start(out=out[:, lo:hi], in_=result[:])

@@ -25,17 +25,20 @@ K_PASS = P * PACK
 PASSES = K // K_PASS
 BLOCKS = K_PASS // 32
 QUADRANT = 32
+QUADRANT_ORDER = (0, 2, 1, 3)
 ROWS = 4
 PER_COLUMN = 16
 LAST = E - 1
 PAIR = 2 * C
 HALF = E // 2
 WA_FIRST = (12, 4)
-H_GROUPS = [(0, 1), (2, 3), (4, 5), (6,), (7,)]
-SCALAR_COPIES = (H_GROUPS[0], H_GROUPS[-1])
+H_GROUPS = [(0, 1), (2, 3), (4,), (5, 6), (7,)]
+VECTOR_COPIES = (3, 4, 5, 6)
 Y_GROUPS = [(0, 1, 2, 3), (4, 5, 6), (7,)]
-OUT_CHUNKS = [(0, 384), (384, T)]
-SUM_BANKS, TURN_BANKS, BASE_BANKS = 4, 3, 1
+OUT_CHUNKS = [(0, 256), (256, T)]
+BANKS, LONG_BANKS = 6, 2
+LAG = 2
+GATHER_GROUPS = [(0,), (1,), (2, 3), (4, 5), (6, 7)]
 
 
 def tile_moe_adp_gelu_kernel(
@@ -48,23 +51,21 @@ def tile_moe_adp_gelu_kernel(
 
         offs_t = keep.tile([P, S // PER_COLUMN], U16, name="offs_t")
         pos_t = [keep.tile([P, T // PER_COLUMN], U16, name="pos%d_t" % r) for r in range(2)]
-        xw = keep.tile([P, PASSES, T], I32, name="xw", align_bytes=64)
+        xw = [keep.tile([P, T], I32, name="xw%d" % s, align_bytes=64) for s in range(PASSES)]
         xs = keep.tile([P, T], U8, name="xs", align_bytes=64)
         wa_last = [keep.tile([P, H], I32, name="wa_last%d" % s, align_bytes=64) for s in range(PASSES)]
-        wa = [keep.tile([P, PASSES, H], I32, name="wa%d" % e, align_bytes=64) for e in range(LAST)]
-        was = [keep.tile([P, HALF, PASSES, H], U8, name="was%d" % a, align_bytes=64) for a in range(2)]
+        wa = [keep.tile([P, PASSES, H], I32, name="wa%d" % e, tag="wa%d" % e, align_bytes=64) for e in range(LAST)]
+        was = keep.tile([P, E // 2, H], U8, name="was", align_bytes=64)
         wb = [keep.tile([P, HALF, N], I32, name="wb%d" % a, align_bytes=64) for a in range(2)]
         wbs = keep.tile([P, E, N], U8, name="wbs", align_bytes=64)
-        w_raw = keep.tile([P, PASSES, PACK, N], F32, name="w_raw")
+        w_raw = [keep.tile([P, PACK, N], F32, name="w_raw%d" % s) for s in range(PASSES)]
         gate_row = keep.tile([P, 2, T // P], F32, name="gate_row")
-        gate_t = [keep.tile([P, T], F32, name="gate%d" % r) for r in range(2)]
         ident = keep.tile([P, P], F32, name="ident")
 
-        nc.gpsimd.memset(xs[:].bitcast(I32), 0)
+        nc.vector.memset(xs[:].bitcast(I32), 0)
         nc.gpsimd.dma_start(out=gate_row[:], in_=gate[:, 0, :].rearrange("r (p c) -> p r c", p=P))
         make_identity(nc, ident[:])
-        for a in range(2):
-            nc.vector.memset(was[a][:].rearrange("p e s i -> p (e s i)").bitcast(I32), 0)
+        nc.vector.memset(was[:].rearrange("p g i -> p (g i)").bitcast(I32), 0)
         nc.vector.memset(wbs[:].rearrange("p e n -> p (e n)").bitcast(I32), 0)
 
         def load_wa(e):
@@ -74,122 +75,182 @@ def tile_moe_adp_gelu_kernel(
                 for s in range(PASSES):
                     nc.sync.dma_start(out=wa_last[s][:], in_=wa_words[e, s].rearrange("p i d -> p (i d)").bitcast(I32))
 
-        def load_wa_scales(a):
-            for r in range(ROWS):
+        def load_wa_scales(g):
+            for q in QUADRANT_ORDER:
                 nc.sync.dma_start(
-                    out=was[a][WA_FIRST[a] + r : P : QUADRANT, :, :, :].rearrange("q e s i -> q (e s) i").bitcast(I32),
-                    in_=wa_scales[HALF * a : HALF * (a + 1), :, r:BLOCKS:ROWS, :]
-                    .rearrange("e s q i -> q (e s) i")
+                    out=was[QUADRANT * q : QUADRANT * q + 2 * PASSES * ROWS, g, :].bitcast(I32),
+                    in_=wa_scales[2 * g : 2 * g + 2, :, ROWS * q : ROWS * (q + 1), :]
+                    .rearrange("e s r i -> (e s) r i")
                     .bitcast(I32),
                 )
 
-        nc.sync.dma_start(out=xw[:], in_=x_words.rearrange("s p t d -> p s (t d)").bitcast(I32))
-        for q in range(P // QUADRANT):
+        def load_x(s):
+            nc.sync.dma_start(out=xw[s][:], in_=x_words[s].rearrange("p t d -> p (t d)").bitcast(I32))
+
+        load_x(0)
+        for q in QUADRANT_ORDER:
             nc.sync.dma_start(
                 out=xs[QUADRANT * q : QUADRANT * q + PASSES * ROWS, :].bitcast(I32),
                 in_=x_scales[:, ROWS * q : ROWS * (q + 1), :].bitcast(I32),
             )
+        load_x(1)
         nc.sync.dma_start(offs_t[:], offs)
-        for a in range(2):
-            load_wa(a)
-            load_wa_scales(a)
+        load_wa(0)
+        load_wa_scales(0)
+        load_wa(1)
         for e in range(2, E):
             load_wa(e)
+            if e % 2 == 0:
+                load_wa_scales(e // 2)
         for r in range(ROWS):
-            nc.sync.dma_start(
+            nc.gpsimd.dma_start(
                 out=wbs[r:P:QUADRANT, :, :].bitcast(I32),
                 in_=wb_scales[:, 0, r:BLOCKS:ROWS, :].rearrange("e q n -> q e n").bitcast(I32),
             )
-        for a in range(2):
+
+        def load_wb(a):
             nc.sync.dma_start(
                 out=wb[a][:],
                 in_=wb_words[HALF * a : HALF * (a + 1)].rearrange("e s p n d -> p (e s) (n d)").bitcast(I32),
             )
-        nc.sync.dma_start(
-            out=w_raw[:].rearrange("p s j n -> p s (j n)"), in_=w.rearrange("(s p j) n -> p s (j n)", s=PASSES, j=PACK)
-        )
+
+        def load_w(s):
+            nc.sync.dma_start(
+                out=w_raw[s][:].rearrange("p j n -> p (j n)"),
+                in_=w[s * K_PASS : (s + 1) * K_PASS, :].rearrange("(p j) n -> p (j n)", j=PACK),
+            )
+
+        load_w(0)
+        load_wb(0)
+        load_wb(1)
+        load_w(1)
         nc.sync.dma_start(pos_t[0][:], pos1)
         nc.sync.dma_start(pos_t[1][:], pos2)
-
-        for r in range(2):
-            spread = psum.tile([P, T // P, P], F32, name="spread%d" % r, tag="turn", bufs=TURN_BANKS)
-            for c in range(T // P):
-                nc.tensor.transpose(spread[:, c, :], gate_row[:, r, c : c + 1].to_broadcast([P, P]), ident[:])
-            nc.vector.tensor_copy(
-                out=gate_t[r][:].rearrange("q (p c) -> q p c", p=P), in_=spread[:].rearrange("q c p -> q p c")
-            )
 
         gw = [
             [keep.tile([P, PAIR], U32, name="gw%d_%d" % (g, s), align_bytes=64) for s in range(PASSES)]
             for g in range(E // 2)
         ]
         gs = [keep.tile([P, PAIR], U8, name="gs%d" % g, align_bytes=64) for g in range(E // 2)]
-        for e in range(E):
-            g, slots = e // 2, slice((e % 2) * C, (e % 2 + 1) * C)
-            picks = offs_t[:, e * C // PER_COLUMN : (e + 1) * C // PER_COLUMN]
-            nc.vector.tensor_copy(gw[g][0][:, slots], xw[:, 0, :].bitcast(U32).indirect(picks))
+        for group in GATHER_GROUPS:
+            e = group[0]
+            g, slots = e // 2, slice((e % 2) * C, (e % 2 + len(group)) * C)
+            picks = offs_t[:, e * C // PER_COLUMN : (e + len(group)) * C // PER_COLUMN]
+            nc.vector.tensor_copy(gw[g][0][:, slots], xw[0][:].bitcast(U32).indirect(picks))
             if e % 2 == 0:
                 pair_picks = offs_t[:, g * PAIR // PER_COLUMN : (g + 1) * PAIR // PER_COLUMN]
                 nc.vector.tensor_copy(gs[g][:], xs[:].indirect(pair_picks))
-            nc.vector.tensor_copy(gw[g][1][:, slots], xw[:, 1, :].bitcast(U32).indirect(picks))
+            nc.vector.tensor_copy(gw[g][1][:, slots], xw[1][:].bitcast(U32).indirect(picks))
 
-        h_rows, turned, h_codes, h_scales = {}, {}, {}, {}
+        h_rows, turned, grouped, h_codes, h_scales = {}, {}, {}, {}, {}
 
-        def first_layer(e):
+        def bank(name):
+            return psum.tile([P, H], F32, name=name, tag="bank", bufs=BANKS)
+
+        def long_bank(name):
+            return psum.tile([P, H], F32, name=name, tag="long", bufs=LONG_BANKS)
+
+        def multiply(e, sums, columns):
             g, slots = e // 2, slice((e % 2) * C, (e % 2 + 1) * C)
-            pre = psum.tile([P, H], F32, name="pre%d" % e, tag="sum", bufs=SUM_BANKS)
             for s in range(PASSES):
-                words = wa[e][:, s, :] if e < LAST else wa_last[s][:]
+                words = wa[e][:, s, columns] if e < LAST else wa_last[s][:, columns]
                 nc.tensor.matmul_mx(
-                    out=pre[:],
+                    out=sums,
                     lhsT=gw[g][s][:, slots].bitcast(FP8X4),
                     lhsT_scale=gs[g][ROWS * s : P, slots],
                     rhs=words.bitcast(FP8X4),
-                    rhs_scale=was[e // HALF][WA_FIRST[e // HALF] : P, e % HALF, s, :],
+                    rhs_scale=was[ROWS * (PASSES * (e % 2) + s) : P, g, columns],
                     start=(s == 0),
                     stop=(s == PASSES - 1),
                 )
+
+        def first_layer(e):
             h_rows[e] = keep.tile([P, H], BF16, name="h_rows%d" % e, align_bytes=64)
             h_view = h_rows[e][:].rearrange("c (u m d) -> c u m d", u=2, d=2)
-            pre_view = pre[:].rearrange("c (m u d) -> c u m d", u=2, d=2)
-            if e < LAST:
-                nc.scalar.activation(out=h_view, in_=pre_view, func=GELU)
-            else:
+            if e < LAG or e == LAST:
+                pre = bank("pre%d" % e)
+                multiply(e, pre[:], slice(0, H))
+                pre_view = pre[:].rearrange("c (m u d) -> c u m d", u=2, d=2)
+                if e < LAG:
+                    nc.scalar.activation(out=h_view, in_=pre_view, func=GELU)
+                    return
                 for u in range(2):
                     nc.scalar.activation(out=h_view[:, u, :, :], in_=pre_view[:, u, :, :], func=GELU)
+                return
+            halves = [bank("pre%d_%d" % (e, half)) for half in range(2)]
+            for half in range(2):
+                multiply(e, halves[half][:, : H // 2], slice(half * H // 2, (half + 1) * H // 2))
+            transposes(e - LAG, halves[1][:, H // 2 :])
+            for half in range(2):
+                nc.scalar.activation(
+                    out=h_view[:, :, half * P // 2 : (half + 1) * P // 2, :],
+                    in_=halves[half][:, : H // 2].rearrange("c (m u d) -> c u m d", u=2, d=2),
+                    func=GELU,
+                )
+            quantise(e - LAG)
 
-        def turn(e):
-            group = [members for members in H_GROUPS if e in members][0]
-            size = len(group)
-            if e == group[0]:
-                turned[group] = psum.tile([P, size, 2, C], F32, name="turned%d" % e, tag="turn", bufs=TURN_BANKS)
+        def transposes(e, room):
+            turned[e] = room.rearrange("p (u c) -> p u c", u=2)
             h_pairs = h_rows[e][:].bitcast(F32)
             for u in range(2):
-                nc.tensor.transpose(turned[group][:, e - group[0], u, :], h_pairs[:, u * P : (u + 1) * P], ident[:])
-            if e != group[-1]:
-                return
-            grouped = keep.tile([P, size * C * PACK], BF16, name="grouped%d" % group[0], align_bytes=64)
-            copy_out = nc.scalar.copy if group in SCALAR_COPIES else nc.vector.tensor_copy
+                nc.tensor.transpose(turned[e][:, u, :], h_pairs[:, u * P : (u + 1) * P], ident[:])
+
+        def quantise(e):
+            group = [members for members in H_GROUPS if e in members][0]
+            size, place = len(group), e - group[0]
+            if place == 0:
+                grouped[group] = keep.tile([P, size * C * PACK], BF16, name="grouped%d" % e, align_bytes=64)
+            copy_out = nc.vector.tensor_copy if e in VECTOR_COPIES else nc.scalar.copy
             copy_out(
-                out=grouped[:].bitcast(F32).rearrange("p (a c u) -> p a c u", a=size, u=2),
-                in_=turned[group][:].rearrange("p a u c -> p a c u"),
+                out=grouped[group][:, place * C * PACK : (place + 1) * C * PACK]
+                .bitcast(F32)
+                .rearrange("p (c u) -> p c u", u=2),
+                in_=turned[e].rearrange("p u c -> p c u"),
             )
+            if e == group[-1]:
+                to_codes(group, grouped[group])
+
+        def to_codes(group, values):
+            size = len(group)
             codes = keep.tile([P, size * C], U32, name="h_codes%d" % group[0], align_bytes=64)
             scales = keep.tile([P, size * C], U8, name="h_scales%d" % group[0], align_bytes=64)
-            nc.vector.quantize_mx(out=codes[:].bitcast(FP8X4), scales=scales[:], in_=grouped[:])
+            nc.vector.quantize_mx(out=codes[:].bitcast(FP8X4), scales=scales[:], in_=values[:])
             for place, member in enumerate(group):
                 h_codes[member] = codes[:, place * C : (place + 1) * C]
                 h_scales[member] = scales[:, place * C : (place + 1) * C]
 
-        first_layer(0)
-        for e in range(1, E):
+        def turn_alone(e):
+            room = bank("turned%d" % e)
+            transposes(e, room[:, : H // 2])
+            quantise(e)
+
+        spread = [long_bank("spread%d" % r)[:].rearrange("q (c p) -> q c p", p=P) for r in range(2)]
+        for r in range(2):
+            for c in range(T // P):
+                nc.tensor.transpose(spread[r][:, c, :], gate_row[:, r, c : c + 1].to_broadcast([P, P]), ident[:])
+        gate_t = []
+        for e in range(LAST):
             first_layer(e)
-            turn(e - 1)
-        turn(LAST)
+            if e < 2:
+                gate_t.append(keep.tile([P, T], F32, name="gate%d" % e, tag="wa%d" % e, align_bytes=64))
+                nc.vector.tensor_copy(
+                    out=gate_t[e][:].rearrange("q (p c) -> q p c", p=P), in_=spread[e].rearrange("q c p -> q p c")
+                )
+        first_layer(LAST)
+        room = bank("turned_late")
+        transposes(LAST - 1, room[:, H // 2 :])
+        transposes(LAST - 2, room[:, : H // 2])
+        late = keep.tile([P, 2 * C * PACK], BF16, name="grouped_late", align_bytes=64)
+        nc.vector.tensor_copy(
+            out=late[:].bitcast(F32).rearrange("p (a c u) -> p a c u", a=2, u=2),
+            in_=room[:].rearrange("p (a u c) -> p a c u", a=2, u=2),
+        )
+        to_codes((LAST - 2, LAST - 1), late)
+        turn_alone(LAST)
 
         y = keep.tile([P, S], F32, name="y")
         for group in Y_GROUPS:
-            acc = psum.tile([P, len(group) * C], F32, name="y_acc%d" % group[0], tag="sum", bufs=SUM_BANKS)
+            acc = (long_bank if group == Y_GROUPS[0] else bank)("y_acc%d" % group[0])
             for place, e in enumerate(group):
                 nc.tensor.matmul_mx(
                     out=acc[:, place * C : (place + 1) * C],
@@ -200,34 +261,36 @@ def tile_moe_adp_gelu_kernel(
                     start=True,
                     stop=True,
                 )
-            nc.scalar.copy(out=y[:, group[0] * C : (group[-1] + 1) * C], in_=acc[:])
+            nc.scalar.copy(out=y[:, group[0] * C : (group[-1] + 1) * C], in_=acc[:, : len(group) * C])
 
-        w_grouped = keep.tile([P, PASSES, N, PACK], BF16, name="w_grouped", align_bytes=64)
-        nc.vector.tensor_copy(out=w_grouped[:], in_=w_raw[:].rearrange("p s j n -> p s n j"))
-        w_codes = keep.tile([P, PASSES * N], U32, name="w_codes", align_bytes=64)
-        w_scales = keep.tile([P, PASSES * N], U8, name="w_scales", align_bytes=64)
-        nc.vector.quantize_mx(
-            out=w_codes[:].bitcast(FP8X4), scales=w_scales[:], in_=w_grouped[:].rearrange("p s n j -> p (s n j)")
-        )
-        base = psum.tile([P, T], F32, name="base", tag="base", bufs=BASE_BANKS)
+        base = long_bank("base")
         for s in range(PASSES):
+            w_grouped = keep.tile([P, N, PACK], BF16, name="w_grouped%d" % s, align_bytes=64)
+            nc.vector.tensor_copy(out=w_grouped[:], in_=w_raw[s][:].rearrange("p j n -> p n j"))
+            w_codes = keep.tile([P, N], U32, name="w_codes%d" % s, align_bytes=64)
+            w_scales = keep.tile([P, N], U8, name="w_scales%d" % s, align_bytes=64)
+            nc.vector.quantize_mx(
+                out=w_codes[:].bitcast(FP8X4), scales=w_scales[:], in_=w_grouped[:].rearrange("p n j -> p (n j)")
+            )
             nc.tensor.matmul_mx(
                 out=base[:],
-                lhsT=w_codes[:, s * N : (s + 1) * N].bitcast(FP8X4),
-                lhsT_scale=w_scales[:, s * N : (s + 1) * N],
-                rhs=xw[:, s, :].bitcast(FP8X4),
+                lhsT=w_codes[:].bitcast(FP8X4),
+                lhsT_scale=w_scales[:],
+                rhs=xw[s][:].bitcast(FP8X4),
                 rhs_scale=xs[ROWS * s : P, :],
                 start=(s == 0),
                 stop=(s == PASSES - 1),
             )
 
-        parts = [[keep.tile([P, hi - lo], F32, name="part%d_%d" % (r, lo)) for r in range(2)] for lo, hi in OUT_CHUNKS]
-        for part, (lo, hi) in zip(parts, OUT_CHUNKS):
-            for r in range(2):
-                places = pos_t[r][:, lo // PER_COLUMN : hi // PER_COLUMN]
-                nc.vector.tensor_tensor(part[r][:], y[:].indirect(places), gate_t[r][:, lo:hi], MULT)
-            routed = keep.tile([P, hi - lo], F32, name="routed%d" % lo)
-            nc.vector.tensor_tensor(routed[:], part[0][:], part[1][:], ADD)
-            result = keep.tile([P, hi - lo], F32, name="result%d" % lo)
-            nc.vector.tensor_tensor(result[:], base[:, lo:hi], routed[:], ADD)
-            nc.sync.dma_start(out=out[:, lo:hi], in_=result[:])
+        parts = [keep.tile([P, T], F32, name="part%d" % r) for r in range(2)]
+        nc.vector.tensor_tensor(parts[0][:], y[:].indirect(pos_t[0][:]), gate_t[0][:], MULT)
+        for lo, hi in OUT_CHUNKS:
+            places = pos_t[1][:, lo // PER_COLUMN : hi // PER_COLUMN]
+            nc.vector.tensor_tensor(parts[1][:, lo:hi], y[:].indirect(places), gate_t[1][:, lo:hi], MULT)
+        routed = keep.tile([P, T], F32, name="routed")
+        for lo, hi in OUT_CHUNKS:
+            nc.vector.tensor_tensor(routed[:, lo:hi], parts[0][:, lo:hi], parts[1][:, lo:hi], ADD)
+        result = keep.tile([P, T], F32, name="result")
+        for lo, hi in OUT_CHUNKS:
+            nc.vector.tensor_tensor(result[:, lo:hi], base[:, lo:hi], routed[:, lo:hi], ADD)
+            nc.sync.dma_start(out=out[:, lo:hi], in_=result[:, lo:hi])

@@ -1,7 +1,6 @@
 from contextlib import ExitStack
 
 import concourse.mybir as mybir
-from concourse.masks import make_identity
 
 K, T, E, C, H, N = 1024, 512, 8, 128, 512, 128
 S = E * C
@@ -18,6 +17,7 @@ FP8X4 = mybir.dt.float8_e4m3fn_x4
 GELU = mybir.ActivationFunctionType.Gelu_apprx_tanh
 MULT = mybir.AluOpType.mult
 ADD = mybir.AluOpType.add
+EQUAL = mybir.AluOpType.is_equal
 
 P = 128
 PACK = 4
@@ -64,9 +64,20 @@ def tile_moe_adp_gelu_kernel(
 
         nc.vector.memset(xs[:].bitcast(I32), 0)
         nc.gpsimd.dma_start(out=gate_row[:], in_=gate[:, 0, :].rearrange("r (p c) -> p r c", p=P))
-        make_identity(nc, ident[:])
         nc.vector.memset(was[:].rearrange("p g i -> p (g i)").bitcast(I32), 0)
         nc.vector.memset(wbs[:].rearrange("p e n -> p (e n)").bitcast(I32), 0)
+
+        ones = keep.tile([P, P], F32, name="ones")
+        counted = keep.tile([P, P], F32, name="counted", align_bytes=64)
+        turned_count = keep.tile([P, P], F32, name="turned_count", align_bytes=64)
+        nc.vector.memset(ones[:], 1.0)
+        nc.vector.tensor_tensor_scan(counted[:], ones[:], ones[:], 0.0, MULT, ADD)
+        nc.vector.transpose(turned_count[:], counted[:])
+        for q in range(P // QUADRANT):
+            rows = slice(QUADRANT * q, QUADRANT * (q + 1))
+            nc.vector.tensor_scalar(
+                ident[rows, :], counted[rows, :], turned_count[rows, QUADRANT * q : QUADRANT * q + 1], None, EQUAL
+            )
 
         def load_wa(e):
             if e < LAST:

@@ -87,8 +87,9 @@ def tile_moe_adp_gelu_kernel(
                     nc.sync.dma_start(out=wa_last[s][:], in_=wa_words[e, s].rearrange("p i d -> p (i d)").bitcast(I32))
 
         def load_wa_scales(g):
+            queue = nc.sync if g < E // 2 - 1 else nc.gpsimd
             for q in QUADRANT_ORDER:
-                nc.sync.dma_start(
+                queue.dma_start(
                     out=was[QUADRANT * q : QUADRANT * q + 2 * PASSES * ROWS, g, :].bitcast(I32),
                     in_=wa_scales[2 * g : 2 * g + 2, :, ROWS * q : ROWS * (q + 1), :]
                     .rearrange("e s r i -> (e s) r i")

@@ -33,11 +33,11 @@ PAIR = 2 * C
 HALF = E // 2
 WA_FIRST = (12, 4)
 H_GROUPS = [(0, 1), (2, 3), (4,), (5, 6), (7,)]
-VECTOR_COPIES = (3, 4, 5, 6)
+VECTOR_COPIES = (0, 1, 2, 3, 4, 5, 6)
 Y_GROUPS = [(0, 1, 2, 3), (4, 5, 6), (7,)]
 OUT_CHUNKS = [(0, 256), (256, T)]
 BANKS, LONG_BANKS = 6, 2
-LAG = 2
+TURNED_BEHIND = [(), (), (), (0, 1), (), (2, 3), (4,), ()]
 GATHER_GROUPS = [(0,), (1,), (2, 3), (4, 5), (6, 7)]
 
 
@@ -149,15 +149,16 @@ def tile_moe_adp_gelu_kernel(
             g, slots = e // 2, slice((e % 2) * C, (e % 2 + len(group)) * C)
             picks = offs_t[:, e * C // PER_COLUMN : (e + len(group)) * C // PER_COLUMN]
             nc.vector.tensor_copy(gw[g][0][:, slots], xw[0][:].bitcast(U32).indirect(picks))
-            if e % 2 == 0:
-                pair_picks = offs_t[:, g * PAIR // PER_COLUMN : (g + 1) * PAIR // PER_COLUMN]
-                nc.vector.tensor_copy(gs[g][:], xs[:].indirect(pair_picks))
+            nc.vector.tensor_copy(gs[g][:, slots], xs[:].indirect(picks))
             nc.vector.tensor_copy(gw[g][1][:, slots], xw[1][:].bitcast(U32).indirect(picks))
 
         h_rows, turned, grouped, h_codes, h_scales = {}, {}, {}, {}, {}
 
+        taken = []
+
         def bank(name):
-            return psum.tile([P, H], F32, name=name, tag="bank", bufs=BANKS)
+            taken.append(name)
+            return psum.tile([P, H], F32, name=name, tag="bank%d" % (len(taken) % BANKS))
 
         def long_bank(name):
             return psum.tile([P, H], F32, name=name, tag="long", bufs=LONG_BANKS)
@@ -179,11 +180,11 @@ def tile_moe_adp_gelu_kernel(
         def first_layer(e):
             h_rows[e] = keep.tile([P, H], BF16, name="h_rows%d" % e, align_bytes=64)
             h_view = h_rows[e][:].rearrange("c (u m d) -> c u m d", u=2, d=2)
-            if e < LAG or e == LAST:
+            if not TURNED_BEHIND[e]:
                 pre = bank("pre%d" % e)
                 multiply(e, pre[:], slice(0, H))
                 pre_view = pre[:].rearrange("c (m u d) -> c u m d", u=2, d=2)
-                if e < LAG:
+                if e < LAST:
                     nc.scalar.activation(out=h_view, in_=pre_view, func=GELU)
                     return
                 for u in range(2):
@@ -192,14 +193,16 @@ def tile_moe_adp_gelu_kernel(
             halves = [bank("pre%d_%d" % (e, half)) for half in range(2)]
             for half in range(2):
                 multiply(e, halves[half][:, : H // 2], slice(half * H // 2, (half + 1) * H // 2))
-            transposes(e - LAG, halves[1][:, H // 2 :])
+            for earlier, half in zip(TURNED_BEHIND[e], (1, 0)):
+                transposes(earlier, halves[half][:, H // 2 :])
             for half in range(2):
                 nc.scalar.activation(
                     out=h_view[:, :, half * P // 2 : (half + 1) * P // 2, :],
                     in_=halves[half][:, : H // 2].rearrange("c (m u d) -> c u m d", u=2, d=2),
                     func=GELU,
                 )
-            quantise(e - LAG)
+            for earlier in TURNED_BEHIND[e]:
+                quantise(earlier)
 
         def transposes(e, room):
             turned[e] = room.rearrange("p (u c) -> p u c", u=2)
@@ -240,14 +243,15 @@ def tile_moe_adp_gelu_kernel(
         for r in range(2):
             for c in range(T // P):
                 nc.tensor.transpose(spread[r][:, c, :], gate_row[:, r, c : c + 1].to_broadcast([P, P]), ident[:])
-        gate_t = []
+        unread = keep.tile([P, 1], F32, name="unread")
+        nc.scalar.activation(out=unread[:], in_=ones[:, 0:1], func=GELU)
+        gate_t = [keep.tile([P, T], F32, name="gate%d" % r) for r in range(2)]
+        for r in range(2):
+            nc.scalar.copy(
+                out=gate_t[r][:].rearrange("q (p c) -> q p c", p=P), in_=spread[r].rearrange("q c p -> q p c")
+            )
         for e in range(LAST):
             first_layer(e)
-            if e < 2:
-                gate_t.append(keep.tile([P, T], F32, name="gate%d" % e, tag="wa%d" % e, align_bytes=64))
-                nc.vector.tensor_copy(
-                    out=gate_t[e][:].rearrange("q (p c) -> q p c", p=P), in_=spread[e].rearrange("q c p -> q p c")
-                )
         first_layer(LAST)
         room = bank("turned_late")
         transposes(LAST - 1, room[:, H // 2 :])

@@ -33,12 +33,12 @@ PAIR = 2 * C
 HALF = E // 2
 WA_FIRST = (12, 4)
 H_GROUPS = [(0, 1), (2, 3), (4,), (5, 6), (7,)]
-VECTOR_COPIES = (0, 1, 2, 3, 4, 5, 6)
+VECTOR_COPIES = (2, 3, 4)
 Y_GROUPS = [(0, 1, 2, 3), (4, 5, 6), (7,)]
 OUT_CHUNKS = [(0, 256), (256, T)]
 BANKS, LONG_BANKS = 6, 2
 TURNED_BEHIND = [(), (), (), (0, 1), (), (2, 3), (4,), ()]
-GATHER_GROUPS = [(0,), (1,), (2, 3), (4, 5), (6, 7)]
+GATHER_GROUPS = [(0,), (1,), (2,), (3,), (4, 5), (6, 7)]
 
 
 def tile_moe_adp_gelu_kernel(
@@ -243,15 +243,14 @@ def tile_moe_adp_gelu_kernel(
         for r in range(2):
             for c in range(T // P):
                 nc.tensor.transpose(spread[r][:, c, :], gate_row[:, r, c : c + 1].to_broadcast([P, P]), ident[:])
-        unread = keep.tile([P, 1], F32, name="unread")
-        nc.scalar.activation(out=unread[:], in_=ones[:, 0:1], func=GELU)
-        gate_t = [keep.tile([P, T], F32, name="gate%d" % r) for r in range(2)]
-        for r in range(2):
-            nc.scalar.copy(
-                out=gate_t[r][:].rearrange("q (p c) -> q p c", p=P), in_=spread[r].rearrange("q c p -> q p c")
-            )
+        gate_t = []
         for e in range(LAST):
             first_layer(e)
+            if e < 2:
+                gate_t.append(keep.tile([P, T], F32, name="gate%d" % e, tag="wa%d" % e, align_bytes=64))
+                nc.vector.tensor_copy(
+                    out=gate_t[e][:].rearrange("q (p c) -> q p c", p=P), in_=spread[e].rearrange("q c p -> q p c")
+                )
         first_layer(LAST)
         room = bank("turned_late")
         transposes(LAST - 1, room[:, H // 2 :])
@@ -299,14 +298,14 @@ def tile_moe_adp_gelu_kernel(
             )
 
         parts = [keep.tile([P, T], F32, name="part%d" % r) for r in range(2)]
+        with_base = keep.tile([P, T], F32, name="with_base")
+        result = keep.tile([P, T], F32, name="result")
         nc.vector.tensor_tensor(parts[0][:], y[:].indirect(pos_t[0][:]), gate_t[0][:], MULT)
         for lo, hi in OUT_CHUNKS:
             places = pos_t[1][:, lo // PER_COLUMN : hi // PER_COLUMN]
             nc.vector.tensor_tensor(parts[1][:, lo:hi], y[:].indirect(places), gate_t[1][:, lo:hi], MULT)
-        routed = keep.tile([P, T], F32, name="routed")
+            if lo == 0:
+                nc.vector.tensor_tensor(with_base[:], base[:], parts[0][:], ADD)
         for lo, hi in OUT_CHUNKS:
-            nc.vector.tensor_tensor(routed[:, lo:hi], parts[0][:, lo:hi], parts[1][:, lo:hi], ADD)
-        result = keep.tile([P, T], F32, name="result")
-        for lo, hi in OUT_CHUNKS:
-            nc.vector.tensor_tensor(result[:, lo:hi], base[:, lo:hi], routed[:, lo:hi], ADD)
+            nc.vector.tensor_tensor(result[:, lo:hi], with_base[:, lo:hi], parts[1][:, lo:hi], ADD)
             nc.sync.dma_start(out=out[:, lo:hi], in_=result[:, lo:hi])

@@ -105,8 +105,8 @@ def tile_moe_adp_gelu_kernel(
                 out=xs[QUADRANT * q : QUADRANT * q + PASSES * ROWS, :].bitcast(I32),
                 in_=x_scales[:, ROWS * q : ROWS * (q + 1), :].bitcast(I32),
             )
-        load_x(1)
         nc.sync.dma_start(offs_t[:], offs)
+        load_x(1)
         load_wa(0)
         load_wa_scales(0)
         load_wa(1)
@@ -248,7 +248,7 @@ def tile_moe_adp_gelu_kernel(
             first_layer(e)
             if e < 2:
                 gate_t.append(keep.tile([P, T], F32, name="gate%d" % e, tag="wa%d" % e, align_bytes=64))
-                nc.vector.tensor_copy(
+                nc.scalar.copy(
                     out=gate_t[e][:].rearrange("q (p c) -> q p c", p=P), in_=spread[e].rearrange("q c p -> q p c")
                 )
         first_layer(LAST)

@@ -51,14 +51,14 @@ def tile_moe_adp_gelu_kernel(
 
         offs_t = keep.tile([P, S // PER_COLUMN], U16, name="offs_t")
         pos_t = [keep.tile([P, T // PER_COLUMN], U16, name="pos%d_t" % r) for r in range(2)]
-        xw = [keep.tile([P, T], I32, name="xw%d" % s, align_bytes=64) for s in range(PASSES)]
-        xs = keep.tile([P, T], U8, name="xs", align_bytes=64)
-        wa_last = [keep.tile([P, H], I32, name="wa_last%d" % s, align_bytes=64) for s in range(PASSES)]
-        wa = [keep.tile([P, PASSES, H], I32, name="wa%d" % e, tag="wa%d" % e, align_bytes=64) for e in range(LAST)]
-        was = keep.tile([P, E // 2, H], U8, name="was", align_bytes=64)
-        wb = [keep.tile([P, HALF, N], I32, name="wb%d" % a, align_bytes=64) for a in range(2)]
-        wbs = keep.tile([P, E, N], U8, name="wbs", align_bytes=64)
-        w_raw = [keep.tile([P, PACK, N], F32, name="w_raw%d" % s) for s in range(PASSES)]
+        xw = [keep.tile([P, T], I32, name="xw%d" % s, align_bytes=256) for s in range(PASSES)]
+        xs = keep.tile([P, T], U8, name="xs", align_bytes=256)
+        wa_last = [keep.tile([P, H], I32, name="wa_last%d" % s, align_bytes=256) for s in range(PASSES)]
+        wa = [keep.tile([P, PASSES, H], I32, name="wa%d" % e, tag="wa%d" % e, align_bytes=256) for e in range(LAST)]
+        was = keep.tile([P, E // 2, H], U8, name="was", align_bytes=256)
+        wb = [keep.tile([P, HALF, N], I32, name="wb%d" % a, align_bytes=256) for a in range(2)]
+        wbs = keep.tile([P, E, N], U8, name="wbs", align_bytes=256)
+        w_raw = [keep.tile([P, PACK, N], F32, name="w_raw%d" % s, align_bytes=256) for s in range(PASSES)]
         gate_row = keep.tile([P, 2, T // P], F32, name="gate_row")
         ident = keep.tile([P, P], F32, name="ident")
 
@@ -100,13 +100,13 @@ def tile_moe_adp_gelu_kernel(
             nc.sync.dma_start(out=xw[s][:], in_=x_words[s].rearrange("p t d -> p (t d)").bitcast(I32))
 
         load_x(0)
-        for q in QUADRANT_ORDER:
-            nc.sync.dma_start(
+        for queue, q in zip((nc.scalar, nc.sync, nc.scalar, nc.sync), QUADRANT_ORDER):
+            queue.dma_start(
                 out=xs[QUADRANT * q : QUADRANT * q + PASSES * ROWS, :].bitcast(I32),
                 in_=x_scales[:, ROWS * q : ROWS * (q + 1), :].bitcast(I32),
             )
-        nc.sync.dma_start(offs_t[:], offs)
         load_x(1)
+        nc.sync.dma_start(offs_t[:], offs)
         load_wa(0)
         load_wa_scales(0)
         load_wa(1)
@@ -247,7 +247,7 @@ def tile_moe_adp_gelu_kernel(
         for e in range(LAST):
             first_layer(e)
             if e < 2:
-                gate_t.append(keep.tile([P, T], F32, name="gate%d" % e, tag="wa%d" % e, align_bytes=64))
+                gate_t.append(keep.tile([P, T], F32, name="gate%d" % e, tag="wa%d" % e, align_bytes=256))
                 nc.scalar.copy(
                     out=gate_t[e][:].rearrange("q (p c) -> q p c", p=P), in_=spread[e].rearrange("q c p -> q p c")
                 )
@@ -299,7 +299,7 @@ def tile_moe_adp_gelu_kernel(
 
         parts = [keep.tile([P, T], F32, name="part%d" % r) for r in range(2)]
         with_base = keep.tile([P, T], F32, name="with_base")
-        result = keep.tile([P, T], F32, name="result")
+        result = keep.tile([P, T], F32, name="result", align_bytes=256)
         nc.vector.tensor_tensor(parts[0][:], y[:].indirect(pos_t[0][:]), gate_t[0][:], MULT)
         for lo, hi in OUT_CHUNKS:
             places = pos_t[1][:, lo // PER_COLUMN : hi // PER_COLUMN]

@@ -28,16 +28,17 @@ QUADRANT = 32
 QUADRANT_ORDER = (0, 2, 1, 3)
 ROWS = 4
 PER_COLUMN = 16
-LAST = E - 1
+LAST = 6
+ORDER = [e for e in range(E) if e != LAST] + [LAST]
 PAIR = 2 * C
 HALF = E // 2
-WA_FIRST = (12, 4)
-H_GROUPS = [(0, 1), (2, 3), (4,), (5, 6), (7,)]
+WB_LOADS = [(0, 4), (4, 6), (7, 8), (6, 7)]
+H_GROUPS = [(0, 1), (2, 3), (4, 5), (7,)]
 VECTOR_COPIES = (2, 3, 4)
-Y_GROUPS = [(0, 1, 2, 3), (4, 5, 6), (7,)]
+Y_GROUPS = [(0, 1, 2, 3), (4, 5), (7,), (LAST,)]
 OUT_CHUNKS = [(0, 256), (256, T)]
 BANKS, LONG_BANKS = 6, 2
-TURNED_BEHIND = [(), (), (), (0, 1), (), (2, 3), (4,), ()]
+TURNED_BEHIND = {3: (0, 1), 5: (2, 3), 7: (4,)}
 GATHER_GROUPS = [(0,), (1,), (2,), (3,), (4, 5), (6, 7)]
 
 
@@ -54,9 +55,9 @@ def tile_moe_adp_gelu_kernel(
         xw = [keep.tile([P, T], I32, name="xw%d" % s, align_bytes=256) for s in range(PASSES)]
         xs = keep.tile([P, T], U8, name="xs", align_bytes=256)
         wa_last = [keep.tile([P, H], I32, name="wa_last%d" % s, align_bytes=256) for s in range(PASSES)]
-        wa = [keep.tile([P, PASSES, H], I32, name="wa%d" % e, tag="wa%d" % e, align_bytes=256) for e in range(LAST)]
+        wa = {e: keep.tile([P, PASSES, H], I32, name="wa%d" % e, tag="wa%d" % e, align_bytes=256) for e in ORDER[:-1]}
         was = keep.tile([P, E // 2, H], U8, name="was", align_bytes=256)
-        wb = [keep.tile([P, HALF, N], I32, name="wb%d" % a, align_bytes=256) for a in range(2)]
+        wb = {lo: keep.tile([P, hi - lo, N], I32, name="wb%d" % lo, align_bytes=256) for lo, hi in WB_LOADS}
         wbs = keep.tile([P, E, N], U8, name="wbs", align_bytes=256)
         w_raw = [keep.tile([P, PACK, N], F32, name="w_raw%d" % s, align_bytes=256) for s in range(PASSES)]
         gate_row = keep.tile([P, 2, T // P], F32, name="gate_row")
@@ -80,15 +81,14 @@ def tile_moe_adp_gelu_kernel(
             )
 
         def load_wa(e):
-            if e < LAST:
+            if e != LAST:
                 nc.sync.dma_start(out=wa[e][:], in_=wa_words[e].rearrange("s p i d -> p s (i d)").bitcast(I32))
             else:
                 for s in range(PASSES):
                     nc.sync.dma_start(out=wa_last[s][:], in_=wa_words[e, s].rearrange("p i d -> p (i d)").bitcast(I32))
 
-        def load_wa_scales(g):
-            queue = nc.sync if g < E // 2 - 1 else nc.gpsimd
-            for q in QUADRANT_ORDER:
+        def load_wa_scales(queue, g, quadrants):
+            for q in quadrants:
                 queue.dma_start(
                     out=was[QUADRANT * q : QUADRANT * q + 2 * PASSES * ROWS, g, :].bitcast(I32),
                     in_=wa_scales[2 * g : 2 * g + 2, :, ROWS * q : ROWS * (q + 1), :]
@@ -107,23 +107,26 @@ def tile_moe_adp_gelu_kernel(
             )
         load_x(1)
         nc.sync.dma_start(offs_t[:], offs)
-        load_wa(0)
-        load_wa_scales(0)
-        load_wa(1)
-        for e in range(2, E):
+        load_wa_scales(nc.gpsimd, E // 2 - 1, QUADRANT_ORDER[2:])
+        for place, e in enumerate(ORDER):
             load_wa(e)
-            if e % 2 == 0:
-                load_wa_scales(e // 2)
+            if place in (0, 2, 4):
+                load_wa_scales(nc.sync, place // 2, QUADRANT_ORDER)
+            if place in (1, 3):
+                load_wa_scales(nc.sync, E // 2 - 1, [QUADRANT_ORDER[place // 2]])
         for r in range(ROWS):
             nc.gpsimd.dma_start(
                 out=wbs[r:P:QUADRANT, :, :].bitcast(I32),
                 in_=wb_scales[:, 0, r:BLOCKS:ROWS, :].rearrange("e q n -> q e n").bitcast(I32),
             )
 
-        def load_wb(a):
+        def load_wb(lo, hi):
+            if hi - lo == 1:
+                nc.sync.dma_start(out=wb[lo][:, 0, :], in_=wb_words[lo, 0].rearrange("p n d -> p (n d)").bitcast(I32))
+                return
             nc.sync.dma_start(
-                out=wb[a][:],
-                in_=wb_words[HALF * a : HALF * (a + 1)].rearrange("e s p n d -> p (e s) (n d)").bitcast(I32),
+                out=wb[lo][:],
+                in_=wb_words[lo:hi].rearrange("e s p n d -> p (e s) (n d)").bitcast(I32),
             )
 
         def load_w(s):
@@ -133,10 +136,12 @@ def tile_moe_adp_gelu_kernel(
             )
 
         load_w(0)
-        load_wb(0)
-        load_wb(1)
         load_w(1)
+        for lo, hi in WB_LOADS[:2]:
+            load_wb(lo, hi)
         nc.sync.dma_start(pos_t[0][:], pos1)
+        for lo, hi in WB_LOADS[2:]:
+            load_wb(lo, hi)
         nc.sync.dma_start(pos_t[1][:], pos2)
 
         gw = [
@@ -166,7 +171,7 @@ def tile_moe_adp_gelu_kernel(
         def multiply(e, sums, columns):
             g, slots = e // 2, slice((e % 2) * C, (e % 2 + 1) * C)
             for s in range(PASSES):
-                words = wa[e][:, s, columns] if e < LAST else wa_last[s][:, columns]
+                words = wa[e][:, s, columns]
                 nc.tensor.matmul_mx(
                     out=sums,
                     lhsT=gw[g][s][:, slots].bitcast(FP8X4),
@@ -180,15 +185,10 @@ def tile_moe_adp_gelu_kernel(
         def first_layer(e):
             h_rows[e] = keep.tile([P, H], BF16, name="h_rows%d" % e, align_bytes=64)
             h_view = h_rows[e][:].rearrange("c (u m d) -> c u m d", u=2, d=2)
-            if not TURNED_BEHIND[e]:
+            if e not in TURNED_BEHIND:
                 pre = bank("pre%d" % e)
                 multiply(e, pre[:], slice(0, H))
-                pre_view = pre[:].rearrange("c (m u d) -> c u m d", u=2, d=2)
-                if e < LAST:
-                    nc.scalar.activation(out=h_view, in_=pre_view, func=GELU)
-                    return
-                for u in range(2):
-                    nc.scalar.activation(out=h_view[:, u, :, :], in_=pre_view[:, u, :, :], func=GELU)
+                nc.scalar.activation(out=h_view, in_=pre[:].rearrange("c (m u d) -> c u m d", u=2, d=2), func=GELU)
                 return
             halves = [bank("pre%d_%d" % (e, half)) for half in range(2)]
             for half in range(2):
@@ -223,13 +223,13 @@ def tile_moe_adp_gelu_kernel(
                 in_=turned[e].rearrange("p u c -> p c u"),
             )
             if e == group[-1]:
-                to_codes(group, grouped[group])
+                to_codes(group, grouped[group][:])
 
         def to_codes(group, values):
             size = len(group)
             codes = keep.tile([P, size * C], U32, name="h_codes%d" % group[0], align_bytes=64)
             scales = keep.tile([P, size * C], U8, name="h_scales%d" % group[0], align_bytes=64)
-            nc.vector.quantize_mx(out=codes[:].bitcast(FP8X4), scales=scales[:], in_=values[:])
+            nc.vector.quantize_mx(out=codes[:].bitcast(FP8X4), scales=scales[:], in_=values)
             for place, member in enumerate(group):
                 h_codes[member] = codes[:, place * C : (place + 1) * C]
                 h_scales[member] = scales[:, place * C : (place + 1) * C]
@@ -244,24 +244,41 @@ def tile_moe_adp_gelu_kernel(
             for c in range(T // P):
                 nc.tensor.transpose(spread[r][:, c, :], gate_row[:, r, c : c + 1].to_broadcast([P, P]), ident[:])
         gate_t = []
-        for e in range(LAST):
+        for e in ORDER[:-1]:
             first_layer(e)
             if e < 2:
                 gate_t.append(keep.tile([P, T], F32, name="gate%d" % e, tag="wa%d" % e, align_bytes=256))
                 nc.scalar.copy(
                     out=gate_t[e][:].rearrange("q (p c) -> q p c", p=P), in_=spread[e].rearrange("q c p -> q p c")
                 )
-        first_layer(LAST)
-        room = bank("turned_late")
-        transposes(LAST - 1, room[:, H // 2 :])
-        transposes(LAST - 2, room[:, : H // 2])
-        late = keep.tile([P, 2 * C * PACK], BF16, name="grouped_late", align_bytes=64)
+        turn_alone(5)
+
+        g, slots = LAST // 2, slice((LAST % 2) * C, (LAST % 2 + 1) * C)
+        scales_by_t = keep.tile([P, PACK, P], U8, name="scales_by_t", align_bytes=64)
         nc.vector.tensor_copy(
-            out=late[:].bitcast(F32).rearrange("p (a c u) -> p a c u", a=2, u=2),
-            in_=room[:].rearrange("p (a u c) -> p a c u", a=2, u=2),
+            out=scales_by_t[:].rearrange("p t m -> p m t"), in_=was[:, g, :].rearrange("p (m t) -> p m t", t=PACK)
         )
-        to_codes((LAST - 2, LAST - 1), late)
-        turn_alone(LAST)
+        pre = bank("pre_last")[:].rearrange("p (t c) -> p t c", t=PACK)
+        for s in range(PASSES):
+            words_by_t = keep.tile([P, PACK, P], I32, name="words_by_t%d" % s, align_bytes=64)
+            nc.vector.tensor_copy(
+                out=words_by_t[:].rearrange("p t m -> p m t"), in_=wa_last[s][:].rearrange("p (m t) -> p m t", t=PACK)
+            )
+            for t in range(PACK):
+                nc.tensor.matmul_mx(
+                    out=pre[:, t, :],
+                    lhsT=words_by_t[:, t, :].bitcast(FP8X4),
+                    lhsT_scale=scales_by_t[ROWS * s : P, t, :],
+                    rhs=gw[g][s][:, slots].bitcast(FP8X4),
+                    rhs_scale=gs[g][ROWS * s : P, slots],
+                    start=(s == 0 and t == 0),
+                    stop=(s == PASSES - 1 and t == PACK - 1),
+                )
+            if s == 0:
+                turn_alone(7)
+        h_last = keep.tile([P, C, PACK], BF16, name="h_last", align_bytes=64)
+        nc.scalar.activation(out=h_last[:], in_=pre.rearrange("p t c -> p c t"), func=GELU)
+        to_codes((LAST,), h_last[:].rearrange("p c t -> p (c t)"))
 
         y = keep.tile([P, S], F32, name="y")
         for group in Y_GROUPS:
@@ -269,16 +286,17 @@ def tile_moe_adp_gelu_kernel(
             for place, e in enumerate(group):
                 nc.tensor.matmul_mx(
                     out=acc[:, place * C : (place + 1) * C],
-                    lhsT=wb[e // HALF][:, e % HALF, :].bitcast(FP8X4),
+                    lhsT=[wb[lo][:, e - lo, :] for lo, hi in WB_LOADS if lo <= e < hi][0].bitcast(FP8X4),
                     lhsT_scale=wbs[:, e, :],
                     rhs=h_codes[e].bitcast(FP8X4),
                     rhs_scale=h_scales[e],
                     start=True,
                     stop=True,
                 )
-            nc.scalar.copy(out=y[:, group[0] * C : (group[-1] + 1) * C], in_=acc[:, : len(group) * C])
+            copy_out = nc.vector.tensor_copy if group == Y_GROUPS[1] else nc.scalar.copy
+            copy_out(out=y[:, group[0] * C : (group[-1] + 1) * C], in_=acc[:, : len(group) * C])
 
-        base = long_bank("base")
+        base = psum.tile([P, H], F32, name="base", tag="bank%d" % (len(taken) % BANKS))
         for s in range(PASSES):
             w_grouped = keep.tile([P, N, PACK], BF16, name="w_grouped%d" % s, align_bytes=64)
             nc.vector.tensor_copy(out=w_grouped[:], in_=w_raw[s][:].rearrange("p j n -> p n j"))

@@ -30,6 +30,7 @@ ROWS = 4
 PER_COLUMN = 16
 LAST = 6
 ORDER = [e for e in range(E) if e != LAST] + [LAST]
+RUN = 2 * T // P
 PAIR = 2 * C
 HALF = E // 2
 WB_LOADS = [(0, 4), (4, 6), (7, 8), (6, 7)]
@@ -60,11 +61,12 @@ def tile_moe_adp_gelu_kernel(
         wb = {lo: keep.tile([P, hi - lo, N], I32, name="wb%d" % lo, align_bytes=256) for lo, hi in WB_LOADS}
         wbs = keep.tile([P, E, N], U8, name="wbs", align_bytes=256)
         w_raw = [keep.tile([P, PACK, N], F32, name="w_raw%d" % s, align_bytes=256) for s in range(PASSES)]
-        gate_row = keep.tile([P, 2, T // P], F32, name="gate_row")
+        gate_row = keep.tile([P, RUN], F32, name="gate_row")
         ident = keep.tile([P, P], F32, name="ident")
 
         nc.vector.memset(xs[:].bitcast(I32), 0)
-        nc.gpsimd.dma_start(out=gate_row[:], in_=gate[:, 0, :].rearrange("r (p c) -> p r c", p=P))
+        runs = gate.rearrange("r q (a c) -> (r q a) c", c=RUN)
+        nc.gpsimd.dma_start(out=gate_row[:], in_=runs[0 : 2 * P * T // RUN : 2 * T // RUN + 1, :])
         nc.vector.memset(was[:].rearrange("p g i -> p (g i)").bitcast(I32), 0)
         nc.vector.memset(wbs[:].rearrange("p e n -> p (e n)").bitcast(I32), 0)
 
@@ -107,13 +109,11 @@ def tile_moe_adp_gelu_kernel(
             )
         load_x(1)
         nc.sync.dma_start(offs_t[:], offs)
-        load_wa_scales(nc.gpsimd, E // 2 - 1, QUADRANT_ORDER[2:])
+        load_wa_scales(nc.gpsimd, E // 2 - 1, QUADRANT_ORDER)
         for place, e in enumerate(ORDER):
             load_wa(e)
             if place in (0, 2, 4):
                 load_wa_scales(nc.sync, place // 2, QUADRANT_ORDER)
-            if place in (1, 3):
-                load_wa_scales(nc.sync, E // 2 - 1, [QUADRANT_ORDER[place // 2]])
         for r in range(ROWS):
             nc.gpsimd.dma_start(
                 out=wbs[r:P:QUADRANT, :, :].bitcast(I32),
@@ -137,11 +137,9 @@ def tile_moe_adp_gelu_kernel(
 
         load_w(0)
         load_w(1)
-        for lo, hi in WB_LOADS[:2]:
+        for lo, hi in WB_LOADS:
             load_wb(lo, hi)
         nc.sync.dma_start(pos_t[0][:], pos1)
-        for lo, hi in WB_LOADS[2:]:
-            load_wb(lo, hi)
         nc.sync.dma_start(pos_t[1][:], pos2)
 
         gw = [
@@ -239,18 +237,19 @@ def tile_moe_adp_gelu_kernel(
             transposes(e, room[:, : H // 2])
             quantise(e)
 
-        spread = [long_bank("spread%d" % r)[:].rearrange("q (c p) -> q c p", p=P) for r in range(2)]
-        for r in range(2):
-            for c in range(T // P):
-                nc.tensor.transpose(spread[r][:, c, :], gate_row[:, r, c : c + 1].to_broadcast([P, P]), ident[:])
-        gate_t = []
+        spread = [long_bank("spread%d" % b)[:].rearrange("q (c p) -> q c p", p=P) for b in range(2)]
+        for c in range(RUN):
+            nc.tensor.transpose(spread[c // 4][:, c % 4, :], gate_row[:, c : c + 1].to_broadcast([P, P]), ident[:])
         for e in ORDER[:-1]:
             first_layer(e)
+            if e == 0:
+                gates = keep.tile([P, 2 * T], F32, name="gates", tag="wa0", align_bytes=256)
             if e < 2:
-                gate_t.append(keep.tile([P, T], F32, name="gate%d" % e, tag="wa%d" % e, align_bytes=256))
                 nc.scalar.copy(
-                    out=gate_t[e][:].rearrange("q (p c) -> q p c", p=P), in_=spread[e].rearrange("q c p -> q p c")
+                    out=gates[:].rearrange("q (p b c) -> q b p c", b=2, c=4)[:, e, :, :],
+                    in_=spread[e].rearrange("q c p -> q p c"),
                 )
+        gate_t = [gates[:, r * T : (r + 1) * T] for r in range(2)]
         turn_alone(5)
 
         g, slots = LAST // 2, slice((LAST % 2) * C, (LAST % 2 + 1) * C)
@@ -318,7 +317,7 @@ def tile_moe_adp_gelu_kernel(
         parts = [keep.tile([P, T], F32, name="part%d" % r) for r in range(2)]
         with_base = keep.tile([P, T], F32, name="with_base")
         result = keep.tile([P, T], F32, name="result", align_bytes=256)
-        nc.vector.tensor_tensor(parts[0][:], y[:].indirect(pos_t[0][:]), gate_t[0][:], MULT)
+        nc.vector.tensor_tensor(parts[0][:], y[:].indirect(pos_t[0][:]), gate_t[0], MULT)
         for lo, hi in OUT_CHUNKS:
             places = pos_t[1][:, lo // PER_COLUMN : hi // PER_COLUMN]
             nc.vector.tensor_tensor(parts[1][:, lo:hi], y[:].indirect(places), gate_t[1][:, lo:hi], MULT)

@@ -109,11 +109,14 @@ def tile_moe_adp_gelu_kernel(
             )
         load_x(1)
         nc.sync.dma_start(offs_t[:], offs)
+        load_wa_scales(nc.gpsimd, E // 2 - 2, QUADRANT_ORDER[2:])
         load_wa_scales(nc.gpsimd, E // 2 - 1, QUADRANT_ORDER)
         for place, e in enumerate(ORDER):
             load_wa(e)
-            if place in (0, 2, 4):
+            if place in (0, 2):
                 load_wa_scales(nc.sync, place // 2, QUADRANT_ORDER)
+            if place == 4:
+                load_wa_scales(nc.sync, place // 2, QUADRANT_ORDER[:2])
         for r in range(ROWS):
             nc.gpsimd.dma_start(
                 out=wbs[r:P:QUADRANT, :, :].bitcast(I32),

@@ -15,6 +15,7 @@ U16 = mybir.dt.uint16
 U8 = mybir.dt.uint8
 FP8X4 = mybir.dt.float8_e4m3fn_x4
 GELU = mybir.ActivationFunctionType.Gelu_apprx_tanh
+COPY = mybir.ActivationFunctionType.Copy
 MULT = mybir.AluOpType.mult
 ADD = mybir.AluOpType.add
 EQUAL = mybir.AluOpType.is_equal
@@ -317,15 +318,19 @@ def tile_moe_adp_gelu_kernel(
                 stop=(s == PASSES - 1),
             )
 
-        parts = [keep.tile([P, T], F32, name="part%d" % r) for r in range(2)]
-        with_base = keep.tile([P, T], F32, name="with_base")
+        first = keep.tile([P, T], F32, name="first")
+        picked = keep.tile([P, T], F32, name="picked")
+        second = keep.tile([P, T], F32, name="second")
+        routed = keep.tile([P, T], F32, name="routed")
         result = keep.tile([P, T], F32, name="result", align_bytes=256)
-        nc.vector.tensor_tensor(parts[0][:], y[:].indirect(pos_t[0][:]), gate_t[0], MULT)
         for lo, hi in OUT_CHUNKS:
-            places = pos_t[1][:, lo // PER_COLUMN : hi // PER_COLUMN]
-            nc.vector.tensor_tensor(parts[1][:, lo:hi], y[:].indirect(places), gate_t[1][:, lo:hi], MULT)
-            if lo == 0:
-                nc.vector.tensor_tensor(with_base[:], base[:], parts[0][:], ADD)
+            columns = slice(lo // PER_COLUMN, hi // PER_COLUMN)
+            nc.vector.tensor_tensor(first[:, lo:hi], y[:].indirect(pos_t[0][:, columns]), gate_t[0][:, lo:hi], MULT)
+            nc.scalar.activation(out=picked[:, lo:hi], in_=y[:].indirect(pos_t[1][:, columns]), func=COPY)
         for lo, hi in OUT_CHUNKS:
-            nc.vector.tensor_tensor(result[:, lo:hi], with_base[:, lo:hi], parts[1][:, lo:hi], ADD)
+            nc.vector.tensor_tensor(second[:, lo:hi], picked[:, lo:hi], gate_t[1][:, lo:hi], MULT)
+        for lo, hi in OUT_CHUNKS:
+            nc.vector.tensor_tensor(routed[:, lo:hi], first[:, lo:hi], second[:, lo:hi], ADD)
+        for lo, hi in OUT_CHUNKS:
+            nc.vector.tensor_tensor(result[:, lo:hi], base[:, lo:hi], routed[:, lo:hi], ADD)
             nc.sync.dma_start(out=out[:, lo:hi], in_=result[:, lo:hi])

@@ -37,8 +37,9 @@ HALF = E // 2
 WB_LOADS = [(0, 4), (4, 6), (7, 8), (6, 7)]
 H_GROUPS = [(0, 1), (2, 3), (4, 5), (7,)]
 VECTOR_COPIES = (2, 3, 4)
-Y_GROUPS = [(0, 1, 2, 3), (4, 5), (7,), (LAST,)]
+Y_GROUPS = [(0, 1), (2, 3), (4, 5), (7,)]
 OUT_CHUNKS = [(0, 256), (256, T)]
+FUSED = 384
 BANKS, LONG_BANKS = 6, 2
 TURNED_BEHIND = {3: (0, 1), 5: (2, 3), 7: (4,)}
 GATHER_GROUPS = [(0,), (1,), (2,), (3,), (4, 5), (6, 7)]
@@ -285,7 +286,7 @@ def tile_moe_adp_gelu_kernel(
 
         y = keep.tile([P, S], F32, name="y")
         for group in Y_GROUPS:
-            acc = (long_bank if group == Y_GROUPS[0] else bank)("y_acc%d" % group[0])
+            acc = (long_bank if group in Y_GROUPS[:LONG_BANKS] else bank)("y_acc%d" % group[0])
             for place, e in enumerate(group):
                 nc.tensor.matmul_mx(
                     out=acc[:, place * C : (place + 1) * C],
@@ -296,41 +297,73 @@ def tile_moe_adp_gelu_kernel(
                     start=True,
                     stop=True,
                 )
-            copy_out = nc.vector.tensor_copy if group == Y_GROUPS[1] else nc.scalar.copy
+            copy_out = nc.vector.tensor_copy if group == Y_GROUPS[2] else nc.scalar.copy
             copy_out(out=y[:, group[0] * C : (group[-1] + 1) * C], in_=acc[:, : len(group) * C])
 
-        base = psum.tile([P, H], F32, name="base", tag="bank%d" % (len(taken) % BANKS))
+        last_banks = []
+        for half, copy_out in enumerate((nc.scalar.copy, nc.vector.tensor_copy)):
+            slots = slice(half * C // 2, (half + 1) * C // 2)
+            acc = bank("y_last%d" % half)
+            last_banks.append("bank%d" % (len(taken) % BANKS))
+            nc.tensor.matmul_mx(
+                out=acc[:, : C // 2],
+                lhsT=wb[LAST][:, 0, :].bitcast(FP8X4),
+                lhsT_scale=wbs[:, LAST, :],
+                rhs=h_codes[LAST][:, slots].bitcast(FP8X4),
+                rhs_scale=h_scales[LAST][:, slots],
+                start=True,
+                stop=True,
+            )
+            copy_out(out=y[:, LAST * C + slots.start : LAST * C + slots.stop], in_=acc[:, : C // 2])
+
+        w_codes, w_scales = [], []
         for s in range(PASSES):
             w_grouped = keep.tile([P, N, PACK], BF16, name="w_grouped%d" % s, align_bytes=64)
             nc.vector.tensor_copy(out=w_grouped[:], in_=w_raw[s][:].rearrange("p j n -> p n j"))
-            w_codes = keep.tile([P, N], U32, name="w_codes%d" % s, align_bytes=64)
-            w_scales = keep.tile([P, N], U8, name="w_scales%d" % s, align_bytes=64)
+            w_codes.append(keep.tile([P, N], U32, name="w_codes%d" % s, align_bytes=64))
+            w_scales.append(keep.tile([P, N], U8, name="w_scales%d" % s, align_bytes=64))
             nc.vector.quantize_mx(
-                out=w_codes[:].bitcast(FP8X4), scales=w_scales[:], in_=w_grouped[:].rearrange("p n j -> p (n j)")
+                out=w_codes[s][:].bitcast(FP8X4), scales=w_scales[s][:], in_=w_grouped[:].rearrange("p n j -> p (n j)")
             )
-            nc.tensor.matmul_mx(
-                out=base[:],
-                lhsT=w_codes[:].bitcast(FP8X4),
-                lhsT_scale=w_scales[:],
-                rhs=xw[s][:].bitcast(FP8X4),
-                rhs_scale=xs[ROWS * s : P, :],
-                start=(s == 0),
-                stop=(s == PASSES - 1),
-            )
+        base = {}
+        for (lo, hi), tag in zip(OUT_CHUNKS, last_banks):
+            base[lo] = psum.tile([P, H], F32, name="base%d" % lo, tag=tag)[:, : hi - lo]
+            for s in range(PASSES):
+                nc.tensor.matmul_mx(
+                    out=base[lo],
+                    lhsT=w_codes[s][:].bitcast(FP8X4),
+                    lhsT_scale=w_scales[s][:],
+                    rhs=xw[s][:, lo:hi].bitcast(FP8X4),
+                    rhs_scale=xs[ROWS * s : P, lo:hi],
+                    start=(s == 0),
+                    stop=(s == PASSES - 1),
+                )
 
         first = keep.tile([P, T], F32, name="first")
-        picked = keep.tile([P, T], F32, name="picked")
+        picked = [keep.tile([P, T], F32, name="picked%d" % r) for r in range(2)]
         second = keep.tile([P, T], F32, name="second")
-        routed = keep.tile([P, T], F32, name="routed")
+        with_base = keep.tile([P, T], F32, name="with_base")
         result = keep.tile([P, T], F32, name="result", align_bytes=256)
+
+        def places(r, lo, hi):
+            return y[:].indirect(pos_t[r][:, lo // PER_COLUMN : hi // PER_COLUMN])
+
+        def times_gate(r, lo, hi):
+            nc.vector.tensor_tensor((first, second)[r][:, lo:hi], picked[r][:, lo:hi], gate_t[r][:, lo:hi], MULT)
+
+        def add_base(lo, hi):
+            nc.vector.tensor_tensor(with_base[:, lo:hi], base[lo], first[:, lo:hi], ADD)
+
+        for r, lo, hi in [(0, FUSED, T), (1, 0, T // 2), (1, T // 2, FUSED), (1, FUSED, T)]:
+            nc.scalar.activation(out=picked[r][:, lo:hi], in_=places(r, lo, hi), func=COPY)
+        for lo, hi in [(0, T // 2), (T // 2, FUSED)]:
+            nc.vector.tensor_tensor(first[:, lo:hi], places(0, lo, hi), gate_t[0][:, lo:hi], MULT)
+        times_gate(0, FUSED, T)
+        add_base(0, T // 2)
+        times_gate(1, 0, T // 2)
+        add_base(T // 2, T)
+        times_gate(1, T // 2, FUSED)
+        times_gate(1, FUSED, T)
         for lo, hi in OUT_CHUNKS:
-            columns = slice(lo // PER_COLUMN, hi // PER_COLUMN)
-            nc.vector.tensor_tensor(first[:, lo:hi], y[:].indirect(pos_t[0][:, columns]), gate_t[0][:, lo:hi], MULT)
-            nc.scalar.activation(out=picked[:, lo:hi], in_=y[:].indirect(pos_t[1][:, columns]), func=COPY)
-        for lo, hi in OUT_CHUNKS:
-            nc.vector.tensor_tensor(second[:, lo:hi], picked[:, lo:hi], gate_t[1][:, lo:hi], MULT)
-        for lo, hi in OUT_CHUNKS:
-            nc.vector.tensor_tensor(routed[:, lo:hi], first[:, lo:hi], second[:, lo:hi], ADD)
-        for lo, hi in OUT_CHUNKS:
-            nc.vector.tensor_tensor(result[:, lo:hi], base[:, lo:hi], routed[:, lo:hi], ADD)
+            nc.vector.tensor_tensor(result[:, lo:hi], with_base[:, lo:hi], second[:, lo:hi], ADD)
             nc.sync.dma_start(out=out[:, lo:hi], in_=result[:, lo:hi])

@@ -119,12 +119,6 @@ def tile_moe_adp_gelu_kernel(
                 load_wa_scales(nc.sync, place // 2, QUADRANT_ORDER)
             if place == 4:
                 load_wa_scales(nc.sync, place // 2, QUADRANT_ORDER[:2])
-        for r in range(ROWS):
-            nc.gpsimd.dma_start(
-                out=wbs[r:P:QUADRANT, :, :].bitcast(I32),
-                in_=wb_scales[:, 0, r:BLOCKS:ROWS, :].rearrange("e q n -> q e n").bitcast(I32),
-            )
-
         def load_wb(lo, hi):
             if hi - lo == 1:
                 nc.sync.dma_start(out=wb[lo][:, 0, :], in_=wb_words[lo, 0].rearrange("p n d -> p (n d)").bitcast(I32))
@@ -142,6 +136,11 @@ def tile_moe_adp_gelu_kernel(
 
         load_w(0)
         load_w(1)
+        for r in range(ROWS):
+            nc.sync.dma_start(
+                out=wbs[r:P:QUADRANT, :, :].bitcast(I32),
+                in_=wb_scales[:, 0, r:BLOCKS:ROWS, :].rearrange("e q n -> q e n").bitcast(I32),
+            )
         for lo, hi in WB_LOADS:
             load_wb(lo, hi)
         nc.sync.dma_start(pos_t[0][:], pos1)

@@ -41,7 +41,7 @@ Y_GROUPS = [(0, 1), (2, 3), (4, 5), (7,)]
 OUT_CHUNKS = [(0, 256), (256, T)]
 FUSED = 384
 BANKS, LONG_BANKS = 6, 2
-TURNED_BEHIND = {3: (0, 1), 5: (2, 3), 7: (4,)}
+TURNED_BEHIND = {3: (0, 1), 4: (2,), 5: (3,), 7: (4,)}
 GATHER_GROUPS = [(0,), (1,), (2,), (3,), (4, 5), (6, 7)]
 
 
@@ -279,7 +279,7 @@ def tile_moe_adp_gelu_kernel(
                 )
             if s == 0:
                 turn_alone(7)
-        h_last = keep.tile([P, C, PACK], BF16, name="h_last", align_bytes=64)
+        h_last = keep.tile([P, C, PACK], BF16, name="h_last", tag="h_last", align_bytes=64)
         nc.scalar.activation(out=h_last[:], in_=pre.rearrange("p t c -> p c t"), func=GELU)
         to_codes((LAST,), h_last[:].rearrange("p c t -> p (c t)"))
 
@@ -319,7 +319,8 @@ def tile_moe_adp_gelu_kernel(
         for s in range(PASSES):
             w_grouped = keep.tile([P, N, PACK], BF16, name="w_grouped%d" % s, align_bytes=64)
             nc.vector.tensor_copy(out=w_grouped[:], in_=w_raw[s][:].rearrange("p j n -> p n j"))
-            w_codes.append(keep.tile([P, N], U32, name="w_codes%d" % s, align_bytes=64))
+            tag = "h_last" if s == PASSES - 1 else "w_codes%d" % s
+            w_codes.append(keep.tile([P, N], U32, name="w_codes%d" % s, tag=tag, align_bytes=64))
             w_scales.append(keep.tile([P, N], U8, name="w_scales%d" % s, align_bytes=64))
             nc.vector.quantize_mx(
                 out=w_codes[s][:].bitcast(FP8X4), scales=w_scales[s][:], in_=w_grouped[:].rearrange("p n j -> p (n j)")

@@ -34,6 +34,7 @@ ORDER = [e for e in range(E) if e != LAST] + [LAST]
 RUN = 2 * T // P
 PAIR = 2 * C
 HALF = E // 2
+EARLY_ROWS = 1
 WB_LOADS = [(0, 4), (4, 6), (7, 8), (6, 7)]
 H_GROUPS = [(0, 1), (2, 3), (4, 5), (7,)]
 VECTOR_COPIES = (2, 3, 4)
@@ -137,7 +138,7 @@ def tile_moe_adp_gelu_kernel(
         load_w(0)
         load_w(1)
         for r in range(ROWS):
-            nc.sync.dma_start(
+            (nc.gpsimd if r < EARLY_ROWS else nc.sync).dma_start(
                 out=wbs[r:P:QUADRANT, :, :].bitcast(I32),
                 in_=wb_scales[:, 0, r:BLOCKS:ROWS, :].rearrange("e q n -> q e n").bitcast(I32),
             )

@@ -60,7 +60,9 @@ def tile_moe_adp_gelu_kernel(
         xs = keep.tile([P, T], U8, name="xs", align_bytes=256)
         wa_last = [keep.tile([P, H], I32, name="wa_last%d" % s, align_bytes=256) for s in range(PASSES)]
         wa = {e: keep.tile([P, PASSES, H], I32, name="wa%d" % e, tag="wa%d" % e, align_bytes=256) for e in ORDER[:-1]}
-        was = keep.tile([P, E // 2, H], U8, name="was", align_bytes=256)
+        was_first = keep.tile([P, H], U8, name="was_first", align_bytes=256)
+        was_later = keep.tile([P, E // 2 - 1, H], U8, name="was_later", align_bytes=256)
+        was = [was_first[:]] + [was_later[:, g, :] for g in range(E // 2 - 1)]
         wb = {lo: keep.tile([P, hi - lo, N], I32, name="wb%d" % lo, align_bytes=256) for lo, hi in WB_LOADS}
         wbs = keep.tile([P, E, N], U8, name="wbs", align_bytes=256)
         w_raw = [keep.tile([P, PACK, N], F32, name="w_raw%d" % s, align_bytes=256) for s in range(PASSES)]
@@ -70,7 +72,7 @@ def tile_moe_adp_gelu_kernel(
         nc.vector.memset(xs[:].bitcast(I32), 0)
         runs = gate.rearrange("r q (a c) -> (r q a) c", c=RUN)
         nc.gpsimd.dma_start(out=gate_row[:], in_=runs[0 : 2 * P * T // RUN : 2 * T // RUN + 1, :])
-        nc.vector.memset(was[:].rearrange("p g i -> p (g i)").bitcast(I32), 0)
+        nc.vector.memset(was_later[:].rearrange("p g i -> p (g i)").bitcast(I32), 0)
         nc.vector.memset(wbs[:].rearrange("p e n -> p (e n)").bitcast(I32), 0)
 
         ones = keep.tile([P, P], F32, name="ones")
@@ -95,10 +97,25 @@ def tile_moe_adp_gelu_kernel(
         def load_wa_scales(queue, g, quadrants):
             for q in quadrants:
                 queue.dma_start(
-                    out=was[QUADRANT * q : QUADRANT * q + 2 * PASSES * ROWS, g, :].bitcast(I32),
+                    out=was[g][QUADRANT * q : QUADRANT * q + 2 * PASSES * ROWS, :].bitcast(I32),
                     in_=wa_scales[2 * g : 2 * g + 2, :, ROWS * q : ROWS * (q + 1), :]
                     .rearrange("e s r i -> (e s) r i")
                     .bitcast(I32),
+                )
+
+        def load_first_scales():
+            for q in QUADRANT_ORDER:
+                nc.sync.dma_start(
+                    out=was_first[QUADRANT * q : QUADRANT * (q + 1), :].bitcast(I32),
+                    in_=wa_scales[0:4, :, ROWS * q : ROWS * (q + 1), :].rearrange("e s r i -> (e s) r i").bitcast(I32),
+                )
+
+        def move_second_scales():
+            for q in QUADRANT_ORDER:
+                middle = QUADRANT * q + QUADRANT // 2
+                nc.sync.dma_start(
+                    out=was[1][QUADRANT * q : middle, :].bitcast(I32),
+                    in_=was_first[middle : QUADRANT * (q + 1), :].bitcast(I32),
                 )
 
         def load_x(s):
@@ -116,8 +133,10 @@ def tile_moe_adp_gelu_kernel(
         load_wa_scales(nc.gpsimd, E // 2 - 1, QUADRANT_ORDER)
         for place, e in enumerate(ORDER):
             load_wa(e)
-            if place in (0, 2):
-                load_wa_scales(nc.sync, place // 2, QUADRANT_ORDER)
+            if place == 0:
+                load_first_scales()
+            if place == 2:
+                move_second_scales()
             if place == 4:
                 load_wa_scales(nc.sync, place // 2, QUADRANT_ORDER[:2])
         def load_wb(lo, hi):
@@ -180,7 +199,7 @@ def tile_moe_adp_gelu_kernel(
                     lhsT=gw[g][s][:, slots].bitcast(FP8X4),
                     lhsT_scale=gs[g][ROWS * s : P, slots],
                     rhs=words.bitcast(FP8X4),
-                    rhs_scale=was[ROWS * (PASSES * (e % 2) + s) : P, g, columns],
+                    rhs_scale=was[g][ROWS * (PASSES * (e % 2) + s) : P, columns],
                     start=(s == 0),
                     stop=(s == PASSES - 1),
                 )
@@ -260,7 +279,7 @@ def tile_moe_adp_gelu_kernel(
         g, slots = LAST // 2, slice((LAST % 2) * C, (LAST % 2 + 1) * C)
         scales_by_t = keep.tile([P, PACK, P], U8, name="scales_by_t", align_bytes=64)
         nc.vector.tensor_copy(
-            out=scales_by_t[:].rearrange("p t m -> p m t"), in_=was[:, g, :].rearrange("p (m t) -> p m t", t=PACK)
+            out=scales_by_t[:].rearrange("p t m -> p m t"), in_=was[g].rearrange("p (m t) -> p m t", t=PACK)
         )
         pre = bank("pre_last")[:].rearrange("p (t c) -> p t c", t=PACK)
         for s in range(PASSES):

@@ -28,13 +28,14 @@ BLOCKS = K_PASS // 32
 QUADRANT = 32
 QUADRANT_ORDER = (0, 2, 1, 3)
 ROWS = 4
+PAIR_ROWS = 2 * PASSES * ROWS
 PER_COLUMN = 16
 LAST = 6
 ORDER = [e for e in range(E) if e != LAST] + [LAST]
 RUN = 2 * T // P
 PAIR = 2 * C
 HALF = E // 2
-EARLY_ROWS = 1
+EARLY_ROWS = 2
 WB_LOADS = [(0, 4), (4, 6), (7, 8), (6, 7)]
 H_GROUPS = [(0, 1), (2, 3), (4, 5), (7,)]
 VECTOR_COPIES = (2, 3, 4)
@@ -94,29 +95,19 @@ def tile_moe_adp_gelu_kernel(
                 for s in range(PASSES):
                     nc.sync.dma_start(out=wa_last[s][:], in_=wa_words[e, s].rearrange("p i d -> p (i d)").bitcast(I32))
 
-        def load_wa_scales(queue, g, quadrants):
-            for q in quadrants:
-                queue.dma_start(
-                    out=was[g][QUADRANT * q : QUADRANT * q + 2 * PASSES * ROWS, :].bitcast(I32),
-                    in_=wa_scales[2 * g : 2 * g + 2, :, ROWS * q : ROWS * (q + 1), :]
-                    .rearrange("e s r i -> (e s) r i")
-                    .bitcast(I32),
-                )
+        def load_wa_scales(queue, g, q, pairs):
+            queue.dma_start(
+                out=was[g][QUADRANT * q : QUADRANT * q + pairs * PAIR_ROWS, :].bitcast(I32),
+                in_=wa_scales[2 * g : 2 * (g + pairs), :, ROWS * q : ROWS * (q + 1), :]
+                .rearrange("e s r i -> (e s) r i")
+                .bitcast(I32),
+            )
 
-        def load_first_scales():
-            for q in QUADRANT_ORDER:
-                nc.sync.dma_start(
-                    out=was_first[QUADRANT * q : QUADRANT * (q + 1), :].bitcast(I32),
-                    in_=wa_scales[0:4, :, ROWS * q : ROWS * (q + 1), :].rearrange("e s r i -> (e s) r i").bitcast(I32),
-                )
-
-        def move_second_scales():
-            for q in QUADRANT_ORDER:
-                middle = QUADRANT * q + QUADRANT // 2
-                nc.sync.dma_start(
-                    out=was[1][QUADRANT * q : middle, :].bitcast(I32),
-                    in_=was_first[middle : QUADRANT * (q + 1), :].bitcast(I32),
-                )
+        def move_wa_scales(g, q):
+            nc.sync.dma_start(
+                out=was[g][QUADRANT * q : QUADRANT * q + PAIR_ROWS, :].bitcast(I32),
+                in_=was[g - 1][QUADRANT * q + PAIR_ROWS : QUADRANT * (q + 1), :].bitcast(I32),
+            )
 
         def load_x(s):
             nc.sync.dma_start(out=xw[s][:], in_=x_words[s].rearrange("p t d -> p (t d)").bitcast(I32))
@@ -129,16 +120,22 @@ def tile_moe_adp_gelu_kernel(
             )
         load_x(1)
         nc.sync.dma_start(offs_t[:], offs)
-        load_wa_scales(nc.gpsimd, E // 2 - 2, QUADRANT_ORDER[2:])
-        load_wa_scales(nc.gpsimd, E // 2 - 1, QUADRANT_ORDER)
+        for q in QUADRANT_ORDER:
+            load_wa_scales(nc.gpsimd, 2, q, 2 if q in QUADRANT_ORDER[:2] else 1)
+        for q in QUADRANT_ORDER[2:]:
+            load_wa_scales(nc.gpsimd, 3, q, 1)
         for place, e in enumerate(ORDER):
             load_wa(e)
             if place == 0:
-                load_first_scales()
+                for q in QUADRANT_ORDER:
+                    load_wa_scales(nc.sync, 0, q, 2)
             if place == 2:
-                move_second_scales()
+                for q in QUADRANT_ORDER:
+                    move_wa_scales(1, q)
             if place == 4:
-                load_wa_scales(nc.sync, place // 2, QUADRANT_ORDER[:2])
+                for q in QUADRANT_ORDER[:2]:
+                    move_wa_scales(3, q)
+
         def load_wb(lo, hi):
             if hi - lo == 1:
                 nc.sync.dma_start(out=wb[lo][:, 0, :], in_=wb_words[lo, 0].rearrange("p n d -> p (n d)").bitcast(I32))

from contextlib import ExitStack

import concourse.mybir as mybir

K, T, E, C, H, N = 1024, 512, 8, 128, 512, 128
S = E * C
FLOPS = 2 * K * N * T + 2 * K * H * S + 2 * H * N * S
BYTES = (K * T + E * K * H + E * H * N) * 33 // 32 + 4 * K * N + 2 * 4 * T + 2 * 128 * (S + 2 * T) // 16 + 4 * N * T

F32 = mybir.dt.float32
BF16 = mybir.dt.bfloat16
I32 = mybir.dt.int32
U32 = mybir.dt.uint32
U16 = mybir.dt.uint16
U8 = mybir.dt.uint8
FP8X4 = mybir.dt.float8_e4m3fn_x4
GELU = mybir.ActivationFunctionType.Gelu_apprx_tanh
COPY = mybir.ActivationFunctionType.Copy
MULT = mybir.AluOpType.mult
ADD = mybir.AluOpType.add
EQUAL = mybir.AluOpType.is_equal

P = 128
PACK = 4
K_PASS = P * PACK
PASSES = K // K_PASS
BLOCKS = K_PASS // 32
QUADRANT = 32
QUADRANT_ORDER = (0, 2, 1, 3)
ROWS = 4
PAIR_ROWS = 2 * PASSES * ROWS
PER_COLUMN = 16
LAST = 6
ORDER = [e for e in range(E) if e != LAST] + [LAST]
RUN = 2 * T // P
PAIR = 2 * C
HALF = E // 2
EARLY_ROWS = 2
WB_LOADS = [(0, 4), (4, 6), (7, 8), (6, 7)]
H_GROUPS = [(0, 1), (2, 3), (4, 5), (7,)]
VECTOR_COPIES = (2, 3, 4)
Y_GROUPS = [(0, 1), (2, 3), (4, 5), (7,)]
OUT_CHUNKS = [(0, 256), (256, T)]
FUSED = 384
BANKS, LONG_BANKS = 6, 2
TURNED_BEHIND = {3: (0, 1), 4: (2,), 5: (3,), 7: (4,)}
GATHER_GROUPS = [(0,), (1,), (2,), (3,), (4, 5), (6, 7)]


def tile_moe_adp_gelu_kernel(
    tc, x_words, x_scales, w, wa_words, wa_scales, wb_words, wb_scales, gate, offs, pos1, pos2, out
):
    nc = tc.nc
    with ExitStack() as ctx:
        keep = ctx.enter_context(tc.tile_pool(name="keep", bufs=1))
        psum = ctx.enter_context(tc.psum_pool(name="psum", bufs=1))

        offs_t = keep.tile([P, S // PER_COLUMN], U16, name="offs_t")
        pos_t = [keep.tile([P, T // PER_COLUMN], U16, name="pos%d_t" % r) for r in range(2)]
        xw = [keep.tile([P, T], I32, name="xw%d" % s, align_bytes=256) for s in range(PASSES)]
        xs = keep.tile([P, T], U8, name="xs", align_bytes=256)
        wa_last = [keep.tile([P, H], I32, name="wa_last%d" % s, align_bytes=256) for s in range(PASSES)]
        wa = {e: keep.tile([P, PASSES, H], I32, name="wa%d" % e, tag="wa%d" % e, align_bytes=256) for e in ORDER[:-1]}
        was_first = keep.tile([P, H], U8, name="was_first", align_bytes=256)
        was_later = keep.tile([P, E // 2 - 1, H], U8, name="was_later", align_bytes=256)
        was = [was_first[:]] + [was_later[:, g, :] for g in range(E // 2 - 1)]
        wb = {lo: keep.tile([P, hi - lo, N], I32, name="wb%d" % lo, align_bytes=256) for lo, hi in WB_LOADS}
        wbs = keep.tile([P, E, N], U8, name="wbs", align_bytes=256)
        w_raw = [keep.tile([P, PACK, N], F32, name="w_raw%d" % s, align_bytes=256) for s in range(PASSES)]
        gate_row = keep.tile([P, RUN], F32, name="gate_row")
        ident = keep.tile([P, P], F32, name="ident")

        nc.vector.memset(xs[:].bitcast(I32), 0)
        runs = gate.rearrange("r q (a c) -> (r q a) c", c=RUN)
        nc.gpsimd.dma_start(out=gate_row[:], in_=runs[0 : 2 * P * T // RUN : 2 * T // RUN + 1, :])
        nc.vector.memset(was_later[:].rearrange("p g i -> p (g i)").bitcast(I32), 0)
        nc.vector.memset(wbs[:].rearrange("p e n -> p (e n)").bitcast(I32), 0)

        ones = keep.tile([P, P], F32, name="ones")
        counted = keep.tile([P, P], F32, name="counted", align_bytes=64)
        turned_count = keep.tile([P, P], F32, name="turned_count", align_bytes=64)
        nc.vector.memset(ones[:], 1.0)
        nc.vector.tensor_tensor_scan(counted[:], ones[:], ones[:], 0.0, MULT, ADD)
        nc.vector.transpose(turned_count[:], counted[:])
        for q in range(P // QUADRANT):
            rows = slice(QUADRANT * q, QUADRANT * (q + 1))
            nc.vector.tensor_scalar(
                ident[rows, :], counted[rows, :], turned_count[rows, QUADRANT * q : QUADRANT * q + 1], None, EQUAL
            )

        def load_wa(e):
            if e != LAST:
                nc.sync.dma_start(out=wa[e][:], in_=wa_words[e].rearrange("s p i d -> p s (i d)").bitcast(I32))
            else:
                for s in range(PASSES):
                    nc.sync.dma_start(out=wa_last[s][:], in_=wa_words[e, s].rearrange("p i d -> p (i d)").bitcast(I32))

        def load_wa_scales(queue, g, q, pairs):
            queue.dma_start(
                out=was[g][QUADRANT * q : QUADRANT * q + pairs * PAIR_ROWS, :].bitcast(I32),
                in_=wa_scales[2 * g : 2 * (g + pairs), :, ROWS * q : ROWS * (q + 1), :]
                .rearrange("e s r i -> (e s) r i")
                .bitcast(I32),
            )

        def move_wa_scales(g, q):
            nc.sync.dma_start(
                out=was[g][QUADRANT * q : QUADRANT * q + PAIR_ROWS, :].bitcast(I32),
                in_=was[g - 1][QUADRANT * q + PAIR_ROWS : QUADRANT * (q + 1), :].bitcast(I32),
            )

        def load_x(s):
            nc.sync.dma_start(out=xw[s][:], in_=x_words[s].rearrange("p t d -> p (t d)").bitcast(I32))

        load_x(0)
        for queue, q in zip((nc.scalar, nc.sync, nc.scalar, nc.sync), QUADRANT_ORDER):
            queue.dma_start(
                out=xs[QUADRANT * q : QUADRANT * q + PASSES * ROWS, :].bitcast(I32),
                in_=x_scales[:, ROWS * q : ROWS * (q + 1), :].bitcast(I32),
            )
        load_x(1)
        nc.sync.dma_start(offs_t[:], offs)
        for q in QUADRANT_ORDER:
            load_wa_scales(nc.gpsimd, 2, q, 2 if q in QUADRANT_ORDER[:2] else 1)
        for q in QUADRANT_ORDER[2:]:
            load_wa_scales(nc.gpsimd, 3, q, 1)
        for place, e in enumerate(ORDER):
            load_wa(e)
            if place == 0:
                for q in QUADRANT_ORDER:
                    load_wa_scales(nc.sync, 0, q, 2)
            if place == 2:
                for q in QUADRANT_ORDER:
                    move_wa_scales(1, q)
            if place == 4:
                for q in QUADRANT_ORDER[:2]:
                    move_wa_scales(3, q)

        def load_wb(lo, hi):
            if hi - lo == 1:
                nc.sync.dma_start(out=wb[lo][:, 0, :], in_=wb_words[lo, 0].rearrange("p n d -> p (n d)").bitcast(I32))
                return
            nc.sync.dma_start(
                out=wb[lo][:],
                in_=wb_words[lo:hi].rearrange("e s p n d -> p (e s) (n d)").bitcast(I32),
            )

        def load_w(s):
            nc.sync.dma_start(
                out=w_raw[s][:].rearrange("p j n -> p (j n)"),
                in_=w[s * K_PASS : (s + 1) * K_PASS, :].rearrange("(p j) n -> p (j n)", j=PACK),
            )

        load_w(0)
        load_w(1)
        for r in range(ROWS):
            (nc.gpsimd if r < EARLY_ROWS else nc.sync).dma_start(
                out=wbs[r:P:QUADRANT, :, :].bitcast(I32),
                in_=wb_scales[:, 0, r:BLOCKS:ROWS, :].rearrange("e q n -> q e n").bitcast(I32),
            )
        for lo, hi in WB_LOADS:
            load_wb(lo, hi)
        nc.sync.dma_start(pos_t[0][:], pos1)
        nc.sync.dma_start(pos_t[1][:], pos2)

        gw = [
            [keep.tile([P, PAIR], U32, name="gw%d_%d" % (g, s), align_bytes=64) for s in range(PASSES)]
            for g in range(E // 2)
        ]
        gs = [keep.tile([P, PAIR], U8, name="gs%d" % g, align_bytes=64) for g in range(E // 2)]
        for group in GATHER_GROUPS:
            e = group[0]
            g, slots = e // 2, slice((e % 2) * C, (e % 2 + len(group)) * C)
            picks = offs_t[:, e * C // PER_COLUMN : (e + len(group)) * C // PER_COLUMN]
            nc.vector.tensor_copy(gw[g][0][:, slots], xw[0][:].bitcast(U32).indirect(picks))
            nc.vector.tensor_copy(gs[g][:, slots], xs[:].indirect(picks))
            nc.vector.tensor_copy(gw[g][1][:, slots], xw[1][:].bitcast(U32).indirect(picks))

        h_rows, turned, grouped, h_codes, h_scales = {}, {}, {}, {}, {}

        taken = []

        def bank(name):
            taken.append(name)
            return psum.tile([P, H], F32, name=name, tag="bank%d" % (len(taken) % BANKS))

        def long_bank(name):
            return psum.tile([P, H], F32, name=name, tag="long", bufs=LONG_BANKS)

        def multiply(e, sums, columns):
            g, slots = e // 2, slice((e % 2) * C, (e % 2 + 1) * C)
            for s in range(PASSES):
                words = wa[e][:, s, columns]
                nc.tensor.matmul_mx(
                    out=sums,
                    lhsT=gw[g][s][:, slots].bitcast(FP8X4),
                    lhsT_scale=gs[g][ROWS * s : P, slots],
                    rhs=words.bitcast(FP8X4),
                    rhs_scale=was[g][ROWS * (PASSES * (e % 2) + s) : P, columns],
                    start=(s == 0),
                    stop=(s == PASSES - 1),
                )

        def first_layer(e):
            h_rows[e] = keep.tile([P, H], BF16, name="h_rows%d" % e, align_bytes=64)
            h_view = h_rows[e][:].rearrange("c (u m d) -> c u m d", u=2, d=2)
            if e not in TURNED_BEHIND:
                pre = bank("pre%d" % e)
                multiply(e, pre[:], slice(0, H))
                nc.scalar.activation(out=h_view, in_=pre[:].rearrange("c (m u d) -> c u m d", u=2, d=2), func=GELU)
                return
            halves = [bank("pre%d_%d" % (e, half)) for half in range(2)]
            for half in range(2):
                multiply(e, halves[half][:, : H // 2], slice(half * H // 2, (half + 1) * H // 2))
            for earlier, half in zip(TURNED_BEHIND[e], (1, 0)):
                transposes(earlier, halves[half][:, H // 2 :])
            for half in range(2):
                nc.scalar.activation(
                    out=h_view[:, :, half * P // 2 : (half + 1) * P // 2, :],
                    in_=halves[half][:, : H // 2].rearrange("c (m u d) -> c u m d", u=2, d=2),
                    func=GELU,
                )
            for earlier in TURNED_BEHIND[e]:
                quantise(earlier)

        def transposes(e, room):
            turned[e] = room.rearrange("p (u c) -> p u c", u=2)
            h_pairs = h_rows[e][:].bitcast(F32)
            for u in range(2):
                nc.tensor.transpose(turned[e][:, u, :], h_pairs[:, u * P : (u + 1) * P], ident[:])

        def quantise(e):
            group = [members for members in H_GROUPS if e in members][0]
            size, place = len(group), e - group[0]
            if place == 0:
                grouped[group] = keep.tile([P, size * C * PACK], BF16, name="grouped%d" % e, align_bytes=64)
            copy_out = nc.vector.tensor_copy if e in VECTOR_COPIES else nc.scalar.copy
            copy_out(
                out=grouped[group][:, place * C * PACK : (place + 1) * C * PACK]
                .bitcast(F32)
                .rearrange("p (c u) -> p c u", u=2),
                in_=turned[e].rearrange("p u c -> p c u"),
            )
            if e == group[-1]:
                to_codes(group, grouped[group][:])

        def to_codes(group, values):
            size = len(group)
            codes = keep.tile([P, size * C], U32, name="h_codes%d" % group[0], align_bytes=64)
            scales = keep.tile([P, size * C], U8, name="h_scales%d" % group[0], align_bytes=64)
            nc.vector.quantize_mx(out=codes[:].bitcast(FP8X4), scales=scales[:], in_=values)
            for place, member in enumerate(group):
                h_codes[member] = codes[:, place * C : (place + 1) * C]
                h_scales[member] = scales[:, place * C : (place + 1) * C]

        def turn_alone(e):
            room = bank("turned%d" % e)
            transposes(e, room[:, : H // 2])
            quantise(e)

        spread = [long_bank("spread%d" % b)[:].rearrange("q (c p) -> q c p", p=P) for b in range(2)]
        for c in range(RUN):
            nc.tensor.transpose(spread[c // 4][:, c % 4, :], gate_row[:, c : c + 1].to_broadcast([P, P]), ident[:])
        for e in ORDER[:-1]:
            first_layer(e)
            if e == 0:
                gates = keep.tile([P, 2 * T], F32, name="gates", tag="wa0", align_bytes=256)
            if e < 2:
                nc.scalar.copy(
                    out=gates[:].rearrange("q (p b c) -> q b p c", b=2, c=4)[:, e, :, :],
                    in_=spread[e].rearrange("q c p -> q p c"),
                )
        gate_t = [gates[:, r * T : (r + 1) * T] for r in range(2)]
        turn_alone(5)

        g, slots = LAST // 2, slice((LAST % 2) * C, (LAST % 2 + 1) * C)
        scales_by_t = keep.tile([P, PACK, P], U8, name="scales_by_t", align_bytes=64)
        nc.vector.tensor_copy(
            out=scales_by_t[:].rearrange("p t m -> p m t"), in_=was[g].rearrange("p (m t) -> p m t", t=PACK)
        )
        pre = bank("pre_last")[:].rearrange("p (t c) -> p t c", t=PACK)
        for s in range(PASSES):
            words_by_t = keep.tile([P, PACK, P], I32, name="words_by_t%d" % s, align_bytes=64)
            nc.vector.tensor_copy(
                out=words_by_t[:].rearrange("p t m -> p m t"), in_=wa_last[s][:].rearrange("p (m t) -> p m t", t=PACK)
            )
            for t in range(PACK):
                nc.tensor.matmul_mx(
                    out=pre[:, t, :],
                    lhsT=words_by_t[:, t, :].bitcast(FP8X4),
                    lhsT_scale=scales_by_t[ROWS * s : P, t, :],
                    rhs=gw[g][s][:, slots].bitcast(FP8X4),
                    rhs_scale=gs[g][ROWS * s : P, slots],
                    start=(s == 0 and t == 0),
                    stop=(s == PASSES - 1 and t == PACK - 1),
                )
            if s == 0:
                turn_alone(7)
        h_last = keep.tile([P, C, PACK], BF16, name="h_last", tag="h_last", align_bytes=64)
        nc.scalar.activation(out=h_last[:], in_=pre.rearrange("p t c -> p c t"), func=GELU)
        to_codes((LAST,), h_last[:].rearrange("p c t -> p (c t)"))

        y = keep.tile([P, S], F32, name="y")
        for group in Y_GROUPS:
            acc = (long_bank if group in Y_GROUPS[:LONG_BANKS] else bank)("y_acc%d" % group[0])
            for place, e in enumerate(group):
                nc.tensor.matmul_mx(
                    out=acc[:, place * C : (place + 1) * C],
                    lhsT=[wb[lo][:, e - lo, :] for lo, hi in WB_LOADS if lo <= e < hi][0].bitcast(FP8X4),
                    lhsT_scale=wbs[:, e, :],
                    rhs=h_codes[e].bitcast(FP8X4),
                    rhs_scale=h_scales[e],
                    start=True,
                    stop=True,
                )
            copy_out = nc.vector.tensor_copy if group == Y_GROUPS[2] else nc.scalar.copy
            copy_out(out=y[:, group[0] * C : (group[-1] + 1) * C], in_=acc[:, : len(group) * C])

        last_banks = []
        for half, copy_out in enumerate((nc.scalar.copy, nc.vector.tensor_copy)):
            slots = slice(half * C // 2, (half + 1) * C // 2)
            acc = bank("y_last%d" % half)
            last_banks.append("bank%d" % (len(taken) % BANKS))
            nc.tensor.matmul_mx(
                out=acc[:, : C // 2],
                lhsT=wb[LAST][:, 0, :].bitcast(FP8X4),
                lhsT_scale=wbs[:, LAST, :],
                rhs=h_codes[LAST][:, slots].bitcast(FP8X4),
                rhs_scale=h_scales[LAST][:, slots],
                start=True,
                stop=True,
            )
            copy_out(out=y[:, LAST * C + slots.start : LAST * C + slots.stop], in_=acc[:, : C // 2])

        w_codes, w_scales = [], []
        for s in range(PASSES):
            w_grouped = keep.tile([P, N, PACK], BF16, name="w_grouped%d" % s, align_bytes=64)
            nc.vector.tensor_copy(out=w_grouped[:], in_=w_raw[s][:].rearrange("p j n -> p n j"))
            tag = "h_last" if s == PASSES - 1 else "w_codes%d" % s
            w_codes.append(keep.tile([P, N], U32, name="w_codes%d" % s, tag=tag, align_bytes=64))
            w_scales.append(keep.tile([P, N], U8, name="w_scales%d" % s, align_bytes=64))
            nc.vector.quantize_mx(
                out=w_codes[s][:].bitcast(FP8X4), scales=w_scales[s][:], in_=w_grouped[:].rearrange("p n j -> p (n j)")
            )
        base = {}
        for (lo, hi), tag in zip(OUT_CHUNKS, last_banks):
            base[lo] = psum.tile([P, H], F32, name="base%d" % lo, tag=tag)[:, : hi - lo]
            for s in range(PASSES):
                nc.tensor.matmul_mx(
                    out=base[lo],
                    lhsT=w_codes[s][:].bitcast(FP8X4),
                    lhsT_scale=w_scales[s][:],
                    rhs=xw[s][:, lo:hi].bitcast(FP8X4),
                    rhs_scale=xs[ROWS * s : P, lo:hi],
                    start=(s == 0),
                    stop=(s == PASSES - 1),
                )

        first = keep.tile([P, T], F32, name="first")
        picked = [keep.tile([P, T], F32, name="picked%d" % r) for r in range(2)]
        second = keep.tile([P, T], F32, name="second")
        with_base = keep.tile([P, T], F32, name="with_base")
        result = keep.tile([P, T], F32, name="result", align_bytes=256)

        def places(r, lo, hi):
            return y[:].indirect(pos_t[r][:, lo // PER_COLUMN : hi // PER_COLUMN])

        def times_gate(r, lo, hi):
            nc.vector.tensor_tensor((first, second)[r][:, lo:hi], picked[r][:, lo:hi], gate_t[r][:, lo:hi], MULT)

        def add_base(lo, hi):
            nc.vector.tensor_tensor(with_base[:, lo:hi], base[lo], first[:, lo:hi], ADD)

        for r, lo, hi in [(0, FUSED, T), (1, 0, T // 2), (1, T // 2, FUSED), (1, FUSED, T)]:
            nc.scalar.activation(out=picked[r][:, lo:hi], in_=places(r, lo, hi), func=COPY)
        for lo, hi in [(0, T // 2), (T // 2, FUSED)]:
            nc.vector.tensor_tensor(first[:, lo:hi], places(0, lo, hi), gate_t[0][:, lo:hi], MULT)
        times_gate(0, FUSED, T)
        add_base(0, T // 2)
        times_gate(1, 0, T // 2)
        add_base(T // 2, T)
        times_gate(1, T // 2, FUSED)
        times_gate(1, FUSED, T)
        for lo, hi in OUT_CHUNKS:
            nc.vector.tensor_tensor(result[:, lo:hi], with_base[:, lo:hi], second[:, lo:hi], ADD)
            nc.sync.dma_start(out=out[:, lo:hi], in_=result[:, lo:hi])
